import numpy as np, ml_dtypes
CORES = [9,25,41,57]
N = 4
BF = ml_dtypes.bfloat16
def gentries(a):
    return np.ascontiguousarray(a.reshape(8, 16, -1).transpose(0, 2, 1)).reshape(8, -1)
def gtable(e):
    e = np.asarray(e); return np.ascontiguousarray(e.reshape(8, -1, 16).transpose(0, 2, 1)).reshape(128, -1).astype(np.int32)
A, B, RO, DB, XM = 1280, 256, 2, 5, (1, 2)
P = 3 * A + B
def tie(L, u, v):
    L[u] = v; L[v] = u
def net(rng, nf, pairs, nb, how=""):
    o = rng.permutation(A); k = 3 * A + rng.permutation(B); L = np.arange(P); e = nf + 2 * pairs
    if how == "ends":
        o = o[(o != 0) & (o != A - 1)]; k = k[(k != 3 * A) & (k != P - 1)]
        o = np.concatenate([o[:e], [0, A - 1], o[e:]]); k = np.concatenate([[3 * A, P - 1], k])
    fr, a, b, bd, w = o[:nf], o[nf:nf + pairs], o[nf + pairs:e], o[e:e + nb], o[e + nb:]
    tie(L, a, b); tie(L, bd, k[:nb])
    if how == "chains":
        j = 0; M = 2 ** DB
        for m, shut in ((M - 1, 0), (M, 0), (M + 1, 0), (2 * M, 0), (1, 0), (1, 1), (3, 1), (M + 1, 0)):
            for i in (1, 2):
                tie(L, i * A + b[j:j + m - 1], i * A + a[j + 1:j + m])
                if shut: tie(L, i * A + b[j + m - 1], i * A + a[j])
            j += m
    if how == "selves": tie(L, A + bd, 2 * A + bd)
    if how == "mates": tie(L, A + bd[:nb // 2], A + bd[nb // 2:nb // 2 * 2])
    h = 0 if how in ("selves", "mates") else min(nb, len(w)) * 3 // 4
    tie(L, w[:h], A + bd[:h])
    idle = L == np.arange(P)
    for i in range(3): idle[i * A + fr] = False
    aux = rng.permutation(A + np.flatnonzero(idle[A:3 * A])); n = len(w) - h
    tie(L, w[h:], aux[:n])
    rest = rng.permutation(np.concatenate([aux[n:], 3 * A + np.flatnonzero(idle[3 * A:])])); n = len(rest) // 2
    tie(L, rest[:n], rest[n:2 * n])
    return L, a, b
def sizes(rng):
    nf = int(rng.integers(A // 8, A // 4 + 1)); nb = int(rng.integers(5 * B // 8, 7 * B // 8 + 1)); nw = int(rng.integers(A // 16, A // 8 + 1))
    return nf, (A - nf - nb - nw) // 2, nb
def blank(rng):
    return np.zeros((N, 8, P), np.int64), rng.integers(0, 16, (N, 8, 16, A)), rng.integers(2, 9, (N, 8, 16, RO))
def manned(v):
    at = v[3 * A:]
    return (at < A) & (v[np.minimum(at, A - 1)] == 3 * A + np.arange(B))
def pack(L, x, t):
    return {"lk": np.stack([gtable(v) for v in L]), "x0": np.ascontiguousarray(x.reshape(N, 128, A)).astype(np.int32), "th": np.ascontiguousarray(t.reshape(N, 128, RO)).astype(np.int32)}
def setup_inputs(rng):
    L, x, t = blank(rng)
    for r in range(N):
        for g in range(8): L[r, g] = net(rng, *sizes(rng))[0]
    return pack(L, x, t)
def setup_inputs_chains(rng):
    L, x, t = blank(rng); M = 2 ** DB
    for r in range(N):
        for g in range(8):
            c = (g + r) % 4; nf, n, nb = sizes(rng)
            if c % 2 == 1:
                L[r, g] = net(rng, nf, n, nb)[0]; continue
            if c == 2:
                n = n + nf // 2; nf = 0; t[r, g, :, 0] = 0; t[r, g, :, 1] = 15
            else: t[r, g, :, 0] = 15
            v, a, b = net(rng, nf, n, nb, "chains")
            to = np.array([i * A + p for i in (1, 2) for p in (a[M - 1], a[3 * M], a[5 * M + 1], a[5 * M + 2], b[5 * M + 3], a[5 * M + 5])])
            k = 3 * A + rng.permutation(np.flatnonzero(v[3 * A:] >= A))[:len(to)]
            v[k] = to; L[r, g] = v
            xa = rng.integers(0, 2, (16, M)); xa[0] = 1
            x[r, g][:, a[M - 1:2 * M - 1]] = xa; x[r, g][:, b[M - 1:2 * M - 1]] = rng.integers(14, 16, (16, M))
            x[r, g][:, a[6 * M + 5]] = 0; x[r, g][:, b[6 * M + 5]] = 15
    return pack(L, x, t)
def setup_inputs_room(rng):
    L, x, t = blank(rng); f = A // 8
    for r in range(0, N, 2):
        for g in range(8):
            n = A // 4
            nf, c = ((f, f // 2), (f, f // 2 + 1), (f, f // 2 - 1), (f, 0), (0, f // 2), (1, f // 2), (f + 1, f // 2), (f + 1, f // 2 + 1))[(g + r) % 8]
            L[r, g], a, b = net(rng, nf, n, 3 * B // 4); t[r, g, :, 0] = 5
            xa = rng.integers(0, 16, (16, n)); xb = xa ^ 1; m = rng.permutation(n)[:c]
            xa[:, m] = xa[:, m] & 7; xb[:, m] = xa[:, m] + 8
            x[r, g][:, a] = xa; x[r, g][:, b] = xb
    for r in range(1, N, 2):
        t[r] = rng.integers(1, 8, (8, 16, RO))
        for g in range(8):
            if g == (r + 3) % 8:
                L[r, g] = net(rng, A // 2, A // 4, 0)[0]; t[r, g, :, 0] = 0; t[r, g, :, 1:] = 15; continue
            if g == (r + 4) % 8:
                L[r, g] = net(rng, 0, A // 2, 0)[0]; t[r, g, :, 0] = 15; t[r, g, :, 1:] = 0; continue
            L[r, g], a, b = net(rng, *sizes(rng)); n = len(a); j = np.arange(n)
            xa = rng.integers(0, 8, (16, n)); xb = xa + t[r, g, :, :1]; i = rng.integers(0, 16, n)
            xb[i, j] = xb[i, j] + rng.integers(-1, 2, n)
            if g == (r + 1) % 8:
                t[r, g] = 0; xb = np.where(rng.random(n) < 0.5, xa, xb)
            if g == (r + 2) % 8:
                t[r, g] = 15; xa = np.zeros((16, n), np.int64); xb = xa + 15; xb[i, j] = 14 + rng.integers(0, 2, n)
            x[r, g][:, a] = xa; x[r, g][:, b] = xb
    return pack(L, x, t)
def setup_inputs_border(rng):
    L, x, t = blank(rng); s = int(rng.integers(0, 8))
    for r in range(N):
        for g in range(8):
            how = ("full", "none", "odd", "selves", "mates", "few", "ends", "")[(g + s) % 8]; nf, n, nb = sizes(rng)
            if how == "full" or (how == "odd" and r % 2 == 1): nb = B
            elif how == "none" or how == "odd": nb = 0
            elif how == "few": nb = B // 8
            L[r, g] = net(rng, nf, (A - nf - nb - A // 16) // 2, nb, how)[0]
    return pack(L, x, t)
def setup_inputs_loose(rng):
    L, x, t = blank(rng); z = int(rng.integers(0, 8))
    for g in range(8):
        kk = 3 * A + rng.permutation(B)
        for r in range(N):
            if g == (z + r) % 8:
                L[r, g] = rng.integers(0, P, P); continue
            nf = sizes(rng)[0]; nb = 7 * B // 8
            v, a, b = net(rng, nf, (A - nf - nb - A // 4) // 2, nb)
            fr = np.flatnonzero(v[:A] == np.arange(A)); w = rng.permutation(np.flatnonzero((v[:A] >= A) & (v[:A] < 3 * A)))
            s = B // 8 + r * (B // 16)
            k = np.concatenate([kk[:B // 8], kk[s:s + B // 8]])
            hold = np.ones(P, bool); hold[k] = False
            m = 3 * A + np.flatnonzero((v[3 * A:] < A) & hold[3 * A:]); bd = v[m]
            kind = np.arange(len(k)) % 4
            v[k] = np.where(kind == 0, rng.choice(w, len(k)), np.where(kind == 1, rng.choice(np.concatenate([a, b]), len(k)), np.where(kind == 2, rng.choice(bd, len(k)), rng.choice(fr, len(k)))))
            n = len(w) // 2; kind = np.arange(n) % 3
            v[w[:n]] = np.where(kind == 0, rng.choice(np.concatenate([a, b]), n), np.where(kind == 1, rng.choice(bd, n), rng.choice(m, n)))
            q = A + rng.permutation(2 * A)[:A // 4]
            v[q] = rng.integers(0, 3, len(q)) * A + rng.choice(np.concatenate([fr, a, b]), len(q))
            L[r, g] = v
    for r in range(N):
        q = r ^ XM[0]
        for g in range(8):
            if r > q or g in ((z + r) % 8, (z + q) % 8): continue
            v = L[r, g]; k = int(rng.choice(np.flatnonzero(manned(v) & manned(L[q, g]))))
            v[A - 1] = 3 * A + k; v[3 * A + k] = 2 * A - 1
            k = 3 * A + rng.permutation(np.flatnonzero(manned(v) & manned(L[q, g])))[:8]; c = np.array(v[k])
            v[A + c[:4]] = c[np.array([1, 2, 0, 3])]
            h = np.array(v[:A]); a = np.flatnonzero((h < A) & (h > np.arange(A)) & (v[np.minimum(h, A - 1)] == np.arange(A)))
            a = rng.permutation(a)[:4]; b = np.array(v[a])
            v[k[4:]] = A + a; v[A + b] = c[4:]; x[r, g][:, b] = x[r, g][:, a] ^ 1
    return pack(L, x, t)
def setup_inputs_spread(rng):
    L, x, t = blank(rng)
    x = np.minimum((np.exp2(4.2 * rng.random((N, 8, 1, A))) * rng.random((N, 8, 16, A))).astype(np.int64), 15)
    t = np.minimum((np.exp2(4 * rng.random((N, 8, 16, RO))) * rng.random((N, 8, 16, RO))).astype(np.int64), 15)
    for r in range(N):
        for g in range(8):
            nf = int(rng.integers(0, A // 2)); nb = int(rng.integers(0, B + 1)); nw = int(rng.integers(0, A // 4))
            L[r, g] = net(rng, nf, (A - nf - nb - nw) // 2, nb)[0]
    return pack(L, x, t)
def check_inputs(d):
    bad = []
    for k, hi in (("lk", P - 1), ("x0", 15), ("th", 15)):
        if np.min(d[k]) < 0 or np.max(d[k]) > hi: bad.append("range of " + k)
    return bad
def meet(L, ph, x, th):
    own = np.arange(P); col = np.arange(A); q = L[:A]; c = np.minimum(q, A - 1)
    pair = (q < A) & (q != col) & (L[c] == col)
    dif = np.abs(x - x[:, c]); near = np.add.reduce(dif, axis=0) < th
    free = np.flatnonzero(q == col)
    a = np.flatnonzero(pair & near); b = q[a]
    u = np.flatnonzero(pair & ~near & (col < q))[:len(free) // 2]; v = q[u]
    f1 = free[0:2 * len(u):2]; f2 = free[1:2 * len(u):2]
    J = np.arange(P); S = np.zeros((16, P), np.int64)
    for i in (1, 2):
        J[i * A + a] = L[i * A + b]; S[:, i * A + a] = (ph[:, i * A + b] + dif[:, a]) & 15
    J[A + u] = v; J[2 * A + u] = f1; J[A + v] = u; J[2 * A + v] = f2
    for k in range(DB):
        S = (S + S[:, J]) & 15; J = J[J]
    to = J[L]; ps = (ph + S[:, L]) & 15
    nl = np.array(to); nph = np.array(ps); nx = np.array(x)
    for new, old in ((u, A + v), (v, A + u), (f1, 2 * A + u), (f2, 2 * A + v)):
        nl[new] = to[old]; nph[:, new] = ps[:, old]
    for e, f in ((A + u, A + v), (2 * A + u, A + f1), (2 * A + v, A + f2), (2 * A + f1, 2 * A + f2)):
        nl[e] = f; nl[f] = e; nph[:, e] = 0; nph[:, f] = 0
    for i in range(3):
        nl[i * A + a] = own[i * A + a]; nph[:, i * A + a] = 0
    nx[:, f1] = (x[:, u] + x[:, v]) & 15; nx[:, f2] = dif[:, u]
    return nl, nph, nx
def border(L, ph, x, m):
    at = L[:, :, 3 * A:]; up = (at < A) & (np.take_along_axis(L, np.minimum(at, A - 1), 2) == 3 * A + np.arange(B))
    nl = np.array(L); nph = np.array(ph); nx = np.array(x)
    for r in range(N):
        q = r ^ m
        for g in range(8):
            k = np.flatnonzero(up[r, g] & up[q, g]); a = at[r, g][k]; b = at[q, g][k]
            rho = np.arange(P); rho[a] = A + a; rho[A + a] = a
            nl[r, g] = rho[L[r, g][rho]]
            n = ph[r, g][:, rho]; s = (ph[r, g][:, 3 * A + k] + ph[q, g][:, 3 * A + k]) & 15
            n[:, 3 * A + k] = s; n[:, A + a] = s; nph[r, g] = n
            nx[r, g][:, a] = x[q, g][:, b]
    return nl, nph, nx
def reference(lk, x0, th):
    L = np.stack([gentries(v) for v in lk]).astype(np.int64); x = x0.astype(np.int64).reshape(N, 8, 16, A); ph = np.zeros((N, 8, 16, P), np.int64)
    t = np.add.reduce(th.astype(np.int64).reshape(N, 8, 16, RO), axis=2)
    for rnd in range(RO):
        for r in range(N):
            for g in range(8):
                L[r, g], ph[r, g], x[r, g] = meet(L[r, g], ph[r, g], x[r, g], t[r, g, rnd])
        L, ph, x = border(L, ph, x, XM[rnd])
    return {"yl": L.astype(np.float32), "yp": ph.reshape(N, 128, P).astype(np.float32).astype(BF), "yx": x.reshape(N, 128, A).astype(np.float32).astype(BF)}

@@ -1,0 +1,740 @@
+import numpy as np
+from concourse.mybir import AluOpType as ALU, ActivationFunctionType as ACT
+
+A, NB, P = 1280, 256, 4096
+XM = (1, 2)
+Z = 4096
+SS = 4104
+KA, KB = 1296, 3856
+
+BF, F32, I32, U16 = "bfloat16", "float32", "int32", "uint16"
+SCRATCH = {}
+for _d, _l in (
+        (I32, "LK:256 THI:2 Q:4360 RP1:256 PI:4 RI:82 HF:82 OD:82"),
+        (BF, "THB:2 LX:8192 JA:4360 JB:4096 KT:4112 RHO0:4608 RHO1:4608 ST:3200 XA:3216 XB:3216 XC:1536 X5:1280 DB:1280 DM:1280 MIX:1280 "
+             "TP:1280 TM:1280 TM2:1280 TT:336 DU:320 X2:320 S1:320 S2:320 EQ:256 VR:512 SX0:256 SX1:256 RX0:256 RX1:256 "
+             "W23:144 W01:144 WD:144 WS:144 WF0:144 WF1:144 W45:144 W67:144 WU:144 ONES:128 TRI:128 DG1:128 DG2:128 DG3:128 FL:164"),
+        (F32, "TH:2 SA:4096 SB:4360 SC:2560 PH:4104 YL:256 SP0:256 RP0:256 SF0:16 SF1:16 RF0:16 RF1:16 R:144 C:20 E:16 HI2:64 HI0:64 "
+              "PR:256 PW:256 CW:880 KW:64 MA:128 MB:128 MC:128 D0:164 SN:164 RK:164 LW:256 L4:256 K4:256 P4:256 L5:256 P5:256 "
+              "W:3040 JAW:160 CL:160 CC:160 AW:128 BW:128"),
+        (U16, "LU:256 L4U:256 L5U:256 P5U:256 JU:800 U:1040 OU:64")):
+    for _x in _l.split():
+        SCRATCH[_x.split(":")[0]] = ("sbuf", [128, int(_x.split(":")[1])], _d)
+PSUM = ("P0", "P1", "P2", "P3", "P4B", "P5B", "PV", "PX")
+for _n in PSUM:
+    SCRATCH[_n] = ("psum", [128, 512], F32)
+SEMAPHORES = ["cv", "ca", "cp", "cg", "sent"] + ["d%d" % i for i in range(110)] + ["arr%d" % i for i in range(6)]
+
+CY, PCY = 0.83e-3, 0.83e-3
+GA, SCA, FIX, BW, LAT = 1.56, 3.8, 0.05, 190e3, 0.06
+TRIES, SLACK = 5000, 0.12
+
+
+def V(n, a, b, s=1):
+    return (n, a, b, s)
+
+
+def width(v):
+    return (v[2] - v[1] + v[3] - 1) // v[3]
+
+
+def narrow(v):
+    return SCRATCH[v[0]][2] in (BF, U16)
+
+
+def build():
+    ops = []
+
+    def add(kind, engs, cost, rd, wr, lat=None, **k):
+        ops.append({"kind": kind, "engs": engs, "cost": cost, "rd": [r for r in rd if isinstance(r, tuple) and r[0] in SCRATCH],
+                    "wr": [w for w in wr if w[0] in SCRATCH], "k": k, "lat": lat or {}})
+
+    def plain(o, i):
+        n = width(o)
+        by = n * (2 if narrow(o) else 4) * 128
+        return {"v": FIX + max(64, n * (0.5 if narrow(o) and narrow(i) else 1)) * CY, "a": 0.1 + max(64, n) * CY,
+                "g": 0.17 + 2 * n * CY, "s": 0.06 + by / BW}
+
+    def ts(o, i, s1, op0, s2=None, op1=None):
+        add("ts", "v", plain(o, i), [i, s1, s2], [o], o=o, i=i, s1=s1, s2=s2, op0=op0, op1=op1)
+
+    def tt(o, a, b, op):
+        c = width(o) * (1 if (a[0] in PSUM or b[0] in PSUM) else 2)
+        add("tt", "v", {"v": FIX + max(64, c) * CY}, [a, b], [o], o=o, a=a, b=b, op=op)
+
+    def cp(o, i, engs="v"):
+        add("cp", engs, plain(o, i), [i], [o], lat={"s": 2.0}, o=o, i=i)
+
+    def aff(o, i, bias=0.0, scale=1.0, engs="av"):
+        add("aff", engs, plain(o, i), [i, bias, scale], [o], o=o, i=i, bias=bias, scale=scale)
+
+    def ab(o, i, bias=0.0):
+        add("abs", "a", plain(o, i), [i, bias], [o], o=o, i=i, bias=bias)
+
+    def ga(o, w, l, engs="av", scale=None):
+        n = width(o)
+        add("ga", engs, {"v": 0.05 + n * GA * CY, "a": 0.065 + n * GA * CY}, [w, l], [o], o=o, w=w, l=l, scale=scale)
+
+    def gat(o, w, l, b, op):
+        add("gat", "v", {"v": 0.05 + width(o) * GA * CY}, [w, l, b], [o], o=o, w=w, l=l, b=b, op=op)
+
+    def sca(w, l, i):
+        add("sca", "v", {"v": 0.05 + width(i) * SCA * CY}, [l, i], [w], w=w, l=l, i=i)
+
+    def wrap(o, t, m):
+        add("wrap", "p", {"p": 0.05 + 16 * max(64, width(o)) * PCY}, [t, V(m, 0, 144)], [o], o=o, t=t, m=m)
+
+    def mm(items, acc):
+        add("mm", "p", {"p": 0.05 + sum(max(64, width(x[0])) for x in items) * PCY}, [x[1] for x in items] + [x[2] for x in items],
+            [x[0] for x in items], items=items, acc=acc)
+
+    def io(o, pat, base, cm):
+        add("iota", "g", {"g": 0.13 + 2 * width(o) * CY}, [], [o], o=o, pat=pat, base=base, cm=cm)
+
+    def zero(o):
+        io(o, [[0, width(o)]], 0, 0)
+
+    def dma(o, i, eng="s"):
+        v = o if o[0] in SCRATCH else i
+        add("cp", eng, {"s": plain(v, v)["s"], "a": 0.06}, [i], [o], lat={"s": 2.0, "a": 2.0}, o=o, i=i, dma=True)
+
+    nr = [0]
+
+    def send(o, i, rnd):
+        by = width(i) * (2 if narrow(i) else 4) * 128
+        add("send", "g", {"g": 0.3}, [i], [o], lat={"g": 2.5 + by / 80e3}, o=o, i=i, rnd=rnd, sem="arr%d" % nr[0])
+        nr[0] += 1
+
+    def c_(j):
+        return V("C", j, j + 1)
+
+    def e_(j):
+        return V("E", j, j + 1)
+
+    def sub_(v, a, b):
+        return V(v[0], v[1] + a, v[1] + b)
+
+    add_, sub, mul, mx, mn, band = ALU.add, ALU.subtract, ALU.mult, ALU.max, ALU.min, ALU.bitwise_and
+    IOT = V("LX", P, 2 * P)
+    X0 = V("Q", 0, A)
+
+    dma(V("LK", 0, 256), ("lk", 0, 256, 1))
+    dma(X0, ("x0", 0, A, 1))
+    dma(V("THI", 0, 2), ("th", 0, 2, 1), "a")
+    io(V("PI", 0, 1), [[0, 1]], 0, 1)
+    io(V("R", 0, 144), [[1, 144]], 0, 0)
+    io(V("PR", 0, 256), [[16, 256]], 0, 1)
+    ts(V("PI", 1, 2), V("PI", 0, 1), 15, band)
+    ts(V("PI", 2, 3), V("PI", 0, 1), 112, band)
+    cp(V("C", 0, 3), V("PI", 0, 3))
+    ts(V("E", 0, 16), V("R", 0, 16), c_(1), ALU.is_equal)
+    ts(V("HI2", 0, 64), V("R", 0, 64), e_(2), mul)
+    ts(V("LX", P, P + 64), V("R", 0, 64), e_(3), mul)
+    n = 64
+    while n < 1024:
+        aff(V("LX", P + n, P + 2 * n), V("LX", P, P + n), bias=V("HI2", n // 64, n // 64 + 1), engs="v")
+        n *= 2
+    for j in (1, 2, 3):
+        aff(V("LX", P + 1024 * j, P + 1024 * (j + 1)), V("LX", P, P + 1024), bias=V("HI2", 16 * j, 16 * j + 1), engs="va")
+    ts(c_(10), e_(0), e_(4), add_, e_(6), add_)
+    ts(c_(11), e_(1), e_(5), add_, e_(7), add_)
+    aff(V("HI0", 0, 64), V("R", 0, 64), scale=c_(10), engs="a")
+    aff(V("MIX", 0, 64), V("R", 0, 64), scale=c_(11), engs="a")
+    n = 64
+    while n < A:
+        m = min(n, A - n)
+        aff(V("MIX", n, n + m), V("MIX", 0, m), bias=V("HI0", n // 64, n // 64 + 1), engs="a")
+        n *= 2
+    ts(c_(3), c_(2), 15.0, add_)
+    for c, h in ((4, 2), (5, 0), (15, 4), (16, 6)):
+        aff(c_(c), e_(h), scale=64.0, bias=e_(h + 1))
+    aff(c_(6), c_(5), scale=-1.0, bias=c_(4))
+    aff(c_(17), c_(15), bias=c_(16))
+    aff(c_(7), e_(2), scale=20.0, bias=e_(8))
+    aff(c_(8), e_(2), scale=20.0, bias=e_(9))
+    ts(c_(12), c_(1), 4.0, ALU.is_lt)
+    aff(c_(13), e_(4), bias=e_(5))
+    aff(c_(14), e_(6), bias=e_(7))
+    WS = V("WS", 0, 144)
+    ts(WS, V("R", 0, 144), c_(3), ALU.is_equal)
+    for m, cl in (("W23", c_(4)), ("W01", c_(5)), ("WD", c_(6)), ("WF0", e_(8)), ("WF1", e_(9)), ("W45", c_(15)), ("W67", c_(16)), ("WU", c_(17))):
+        aff(V(m, 0, 144), WS, scale=cl)
+    R8, MA, MB, MC = V("R", 0, 128), V("MA", 0, 128), V("MB", 0, 128), V("MC", 0, 128)
+    ONES, TRI, FL = V("ONES", 0, 128), V("TRI", 0, 128), V("FL", 0, 164)
+    ts(MA, R8, c_(0), ALU.is_equal)
+    for j in (1, 2, 3):
+        aff(V("DG%d" % j, 0, 128), MA, scale=c_(11 + j))
+    aff(c_(18), c_(2), scale=-1.0, bias=-7.5)
+    ab(MB, R8, c_(18))
+    ts(ONES, MB, 8.0, ALU.is_lt)
+    aff(MC, ONES, scale=-1.0)
+    add("tri", "g", plain(TRI, MC), [MC], [TRI], o=TRI, i=MC)
+    ts(V("PW", 0, 256), V("PR", 0, 256), c_(2), sub)
+    col, col2A = V("PW", 0, 80), V("PW", 160, 240)
+    B1, B2, colcol = V("CW", 0, 80), V("CW", 80, 160), V("CW", 160, 320)
+    aff(V("CW", 0, 160), V("PW", 80, 240), bias=4096.0)
+    cp(V("CW", 160, 240), col, "avg")
+    cp(V("CW", 240, 320), col, "avg")
+    cm2A, cmA, cm1296, c2m = V("CW", 320, 400), V("CW", 400, 480), V("CW", 480, 560), V("CW", 800, 880)
+    aff(cm2A, col, bias=-2.0 * A)
+    aff(cmA, col, bias=-1.0 * A)
+    aff(cm1296, col, bias=-1296.0)
+    aff(c2m, col, bias=-2.0 * A, scale=2.0)
+    aff(V("CW", 560, 800), V("PW", 0, 240), bias=float(Z), scale=-1.0)
+    for j, b in enumerate((4096.0, 4352.0, 1280.0, float(SS))):
+        aff(V("KW", 16 * j, 16 * j + 16), V("PW", 0, 16), bias=b)
+    zero(FL)
+    io(V("FL", 0, 1), [[0, 1]], 80, 0)
+    io(V("FL", 82, 83), [[0, 1]], 160, 0)
+    io(V("D0", 0, 164), [[0, 164]], 1, 0)
+    zero(V("D0", 82, 83))
+    cp(V("THB", 0, 2), V("THI", 0, 2))
+    mm([(V("P5B", 0, 2), ONES, V("THB", 0, 2))], False)
+    cp(V("TH", 0, 2), V("P5B", 0, 2), "a")
+    for v in (V("XA", 2560, 2576), V("ST", 0, 1600), V("ST", 1600, 3200), V("LX", 3840, P), V("SA", 0, A), V("SA", 3840, P), V("SB", 0, A),
+              V("SB", 3840, SS), V("KT", A, KA), V("PH", P, SS), V("JA", P, SS), V("XB", A, 1536), V("XB", 2560, 2576),
+              V("XC", A, 1536), V("TT", 320, 336)):
+        zero(v)
+
+    cu = V("U", 0, 80)
+    cp(V("LU", 0, 256), V("LK", 0, 256))
+    ts(cu, V("LK", 0, 80), 1279, mn)
+    cp(V("LW", 0, 256), V("LK", 0, 256), "vg")
+    for j in range(6):
+        ga(V("LX", 640 * j, 640 * (j + 1)), IOT, V("LU", 40 * j, 40 * j + 40))
+    for a in (0, 640):
+        cp(V("XA", a, a + 640), V("Q", a, a + 640), "vg")
+
+    wi = [0]
+
+    def w_():
+        wi[0] += 1
+        return V("W", 80 * (wi[0] - 1), 80 * wi[0])
+
+    for rnd in range(2):
+        wi[0] = 0
+        X, XN = (("XA", "XB"), ("XB", "XC"))[rnd]
+        RHO = "RHO%d" % rnd
+        q, free, cand = V("LW", 0, 80), V("FL", 1, 81), V("FL", 83, 163)
+        ann, pf, dbl, act, spec = (V("PV", 80 * j, 80 * j + 80) for j in range(5))
+        px = [V("PX", 164 + 80 * j, 244 + 80 * j) for j in range(4)]
+        xw, xi = (X0, V("XA", 0, A)) if rnd == 0 else (V("XB", 0, A), V("X5", 0, A))
+        for h in range(2):
+            a, b = 640 * h, 640 * h + 640
+            gat(V("DB", a, b), xw, sub_(cu, 40 * h, 40 * h + 40), sub_(xi, a, b), sub)
+            ab(V(X, A + a, A + b), V("DB", a, b))
+            ga(V("TP", a, b), V("LX", 0, A), sub_(cu, 40 * h, 40 * h + 40))
+        wrap(V("P0", 0, 80), V("TP", 0, A), "W23")
+        wrap(V("P1", 0, 80), V(X, A, 2 * A), "WS")
+        qa, gt, colx, e1, pair, isV, fus = (w_() for _ in range(7))
+        tt(free, q, col, ALU.is_equal)
+        tt(qa, q, col, sub)
+        ts(gt, qa, 0.0, ALU.is_gt)
+        ts(px[0], q, float(A), ALU.is_ge, 8192.0, mul)
+        tt(colx, px[0], col, add_)
+        tt(px[1], V("P0", 0, 80), colx, ALU.is_equal)
+        tt(pair, px[1], free, sub)
+        ts(px[0], V("P1", 0, 80), V("TH", rnd, rnd + 1), ALU.is_lt)
+        tt(ann, px[0], pair, mul)
+        tt(pf, ann, pair, ALU.is_lt)
+        tt(cand, pf, gt, mul)
+        mm([(V("P2", 0, 164), ONES, FL), (V("P2", 200, 364), TRI, FL)], False)
+        add("scan", "v", {"v": FIX + 164 * CY}, [V("D0", 0, 164), V("P2", 0, 164)], [V("SN", 0, 164)], o=V("SN", 0, 164), a=V("D0", 0, 164), b=V("P2", 0, 164))
+        tt(V("RK", 0, 164), V("P2", 200, 364), V("SN", 0, 164), add_)
+        valF = V("RK", 1, 81)
+        offu = V("U", 160, 240)
+        tt(V("PX", 0, 164), V("RK", 0, 164), FL, mul)
+        o1, o2 = w_(), w_()
+        tt(o1, V("PX", 1, 81), col, mx)
+        tt(o2, V("PX", 83, 163), o1, mx)
+        cp(offu, o2)
+        add("cp", "s", {"s": 0.25}, [V("LX", 0, A)], [V("MIX", 0, A)], lat={"s": 2.0}, rows=True)
+        sca(V("ST", 0, 3200), offu, V("MIX", 0, A))
+        if rnd == 0:
+            for t, a, b, c in (("JA", 0, A, 0), ("JA", 3840, P, 3840), ("JB", 0, A, 0), ("JB", 3840, P, 3840), ("RHO0", 0, 2048, 0), ("RHO0", 2048, P, 2048),
+                               ("RHO0", P, 4608, 0), ("RHO1", 0, 2048, 0), ("RHO1", 2048, P, 2048), ("RHO1", P, 4608, 0)):
+                dma(V(t, a, b), V("LX", P + c, P + c + b - a))
+                ops[-1]["rd"].append(V("MIX", 0, 8))
+        mm([(V("P0", 0, 320), V("DG1", 0, 128), V("ST", 2560, 2880)), (V("P0", 0, 320), V("DG2", 0, 128), V("ST", 1280, 1920, 2)),
+            (V("P0", 0, 320), V("DG3", 0, 128), V("ST", 1281, 1920, 2))], True)
+        cp(V("TT", 0, 320), V("P0", 0, 320), "a")
+        tt(isV, pf, cand, sub)
+        qm, qamA, qaA = w_(), w_(), w_()
+        aff(qm, qa, bias=-4096.0)
+        aff(qamA, qa, bias=-1.0 * A)
+        aff(qaA, qa, bias=1.0 * A)
+        tt(e1, ann, qm, mul)
+        tt(V("JAW", 0, 80), e1, B1, add_)
+        tt(V("JAW", 80, 160), e1, B2, add_)
+        dl, dlu = w_(), V("U", 240, 320)
+        tt(dl, ann, cmA, mul)
+        ts(dlu, dl, float(A), add_)
+        if rnd == 0:
+            ga(V("SA", A, 2 * A), V(X, A, 2576), dlu)
+            cp(V("SA", 2 * A, 3 * A), V("SA", A, 2 * A), "sga")
+            for c in range(2):
+                cp(V("SC", 640 * c, 640 * c + 640), V("SA", A + 640 * c, A + 640 * c + 640), "gsa")
+        else:
+            slu = V("U", 320, 480)
+            ts(slu, V("JAW", 0, 160), float(Z), mn)
+            ga(V("DM", 0, A), V(X, A, 2576), dlu)
+            for c in range(4):
+                o = V("SA", A + 640 * c, A + 640 * c + 640)
+                gat(o, V("PH", 0, SS), sub_(slu, 40 * c, 40 * c + 40), V("DM", 640 * (c % 2), 640 * (c % 2) + 640), add_)
+                cp(V("SC", 640 * c, 640 * c + 640), o, "sga" if c % 2 else "gsa")
+        cp(V("RI", 0, 81), V("RK", 1, 82))
+        ts(V("HF", 0, 81), V("RI", 0, 81), 1, ALU.arith_shift_right)
+        ts(V("OD", 0, 80), V("RI", 0, 80), 1, band)
+        odd, lim = V("OD", 0, 80), c_(9)
+        ts(lim, V("HF", 80, 81), 1920.0, add_, V("RK", 163, 164), mn)
+        nFm, nUF, t1, t2, dU, x1, s1 = (w_() for _ in range(7))
+        tlu = V("U", 560, 640)
+        ts(px[0], V("HF", 0, 80), 1920.0, add_)
+        tt(nFm, px[0], free, mul)
+        tt(nUF, V("PX", 83, 163), nFm, add_)
+        ts(act, nUF, lim, ALU.is_lt)
+        aff(t1, nUF, bias=-2880.0)
+        tt(t2, act, t1, mul)
+        ts(tlu, t2, 320.0, add_)
+        tt(dU, act, cand, mul)
+        tt(fus, act, free, mul)
+        tt(s1, ann, fus, add_)
+        for h in range(2):
+            ga(V("TM", 640 * h, 640 * h + 640), V("TT", 0, 336), sub_(tlu, 40 * h, 40 * h + 40))
+        for h in range(2):
+            ga(V("TM2", 640 * h, 640 * h + 640), V("TM", 0, A), sub_(cu, 40 * h, 40 * h + 40))
+        wrap(V("P0", 0, 80), V("TM", 0, A), "W45")
+        wrap(V("P1", 0, 80), V("TM2", 0, A), "W67")
+        tt(x1, V("P0", 0, 80), cand, mul)
+        tt(px[0], V("P1", 0, 80), isV, mul)
+        ts(px[1], px[0], 0.0, ALU.is_gt)
+        tt(dbl, px[1], dU, add_)
+        j1, j2, e3, ju = w_(), w_(), w_(), V("U", 640, 800)
+        tt(px[2], dbl, qamA, mul)
+        tt(j1, px[2], V("JAW", 0, 80), add_)
+        cp(sub_(ju, 0, 80), j1)
+        tt(x1, x1, col2A, sub)
+        tt(e3, px[0], x1, add_)
+        tt(px[1], dbl, e3, mul)
+        tt(j2, px[1], V("JAW", 80, 160), add_)
+        cp(sub_(ju, 80, 160), j2)
+        for h in range(4):
+            ga(V("JA", A + 640 * h, A + 640 * h + 640), V("LX", 0, 2 * P), sub_(ju, 40 * h, 40 * h + 40))
+        tt(spec, dbl, s1, add_)
+        wrap(V("P2", 0, 80), V("TM", 0, A), "W01")
+        wrap(V("P3", 0, 80), V("TM", 0, A), "WD")
+        wrap(V("P4B", 0, 80), V("TM", 0, A), "WU")
+        g1, e5, g12, aq, l4, pa, b1, b2 = (w_() for _ in range(8))
+        tt(b1, V("P3", 0, 80), odd, mul)
+        tt(b2, V("P2", 0, 80), b1, add_)
+        aff(e5, e3, bias=3.0 * A)
+        tt(px[0], b2, cm2A, sub)
+        tt(b1, px[0], fus, mul)
+        tt(px[1], dbl, qaA, mul)
+        tt(g12, px[1], b1, add_)
+        tt(aq, ann, qa, mul)
+        tt(l4, col, g12, add_)
+        l4u = V("U", 800, 880)
+        cp(l4u, l4)
+        ga(V("TP", 0, A), V("LX", 0, P), l4u)
+        wrap(V("P1", 0, 80), V("TP", 0, A), "W23")
+        cp(V("L4U", 0, 80), V("P1", 0, 80))
+        tt(V("CL", 0, 160), colcol, V("LW", 80, 240), sub)
+        tt(px[2], spec, V("CL", 0, 80), mul)
+        tt(px[3], spec, V("CL", 80, 160), mul)
+        tt(V("L4", 80, 240), V("PX", 324, 484), V("LW", 80, 240), add_)
+        cp(V("L4U", 80, 240), V("L4", 80, 240))
+        cp(V("L4U", 240, 256), V("LW", 240, 256))
+        tt(px[0], V("P4B", 0, 80), c2m, sub)
+        tt(pa, px[0], fus, mul)
+        tt(px[1], dbl, e5, mul)
+        tt(g1, px[1], pa, add_)
+        ts(px[0], ann, float(A), mul)
+        ts(px[1], ann, 2.0 * A, mul)
+        tt(V("CC", 0, 80), px[0], g12, add_)
+        tt(V("CC", 80, 160), px[1], g1, add_)
+        if rnd == 0:
+            cp(V("L4", 0, 80), V("P1", 0, 80))
+            PL, pb = "L4", V("LW", 240, 256)
+        else:
+            tt(px[0], ann, V("CW", 560, 640), mul)
+            tt(V("P4", 0, 80), px[0], l4, add_)
+            tt(px[2], spec, V("CW", 640, 720), mul)
+            tt(px[3], spec, V("CW", 720, 800), mul)
+            tt(V("P4", 80, 240), V("PX", 324, 484), V("PW", 80, 240), add_)
+            cp(V("P5U", 160, 240), V("P4", 160, 240))
+            PL, pb = "P4", V("PW", 240, 256)
+        uu = V("U", 880, 900)
+        wrap(V("P5B", 0, 20), V("ST", 2560, 2880), "W01")
+        cp(uu, V("P5B", 0, 20))
+        ga(V("DU", 0, 320), V("DB", 0, A), uu)
+        ga(V("X2", 0, 320), V(X, 0, A), uu, scale=2.0)
+        ab(V(X, 2577, 3216, 2), V("DU", 0, 320))
+        tt(V("S1", 0, 320), V("DU", 0, 320), V("X2", 0, 320), add_)
+        ts(V("S2", 0, 320), V("S1", 0, 320), 16.0, ALU.is_ge, -16.0, mul)
+        tt(V(X, 2576, 3216, 2), V("S1", 0, 320), V("S2", 0, 320), add_)
+        xl, xm, xlu = w_(), w_(), V("U", 900, 980)
+        tt(px[0], valF, cm1296, sub)
+        tt(xl, px[0], fus, mul)
+        tt(xm, xl, col, add_)
+        cp(xlu, xm)
+        ga(V(XN, 0, A), V(X, 0, 3216), xlu)
+        banks = ("P3", "P4B", "P5B", "P2")
+        for s in range(5):
+            jx, jy = ("JA", "JB") if s % 2 == 0 else ("JB", "JA")
+            sx, sy = ("SA", "SB") if s % 2 == 0 else ("SB", "SA")
+            for h in range(2):
+                bk = banks[(2 * s + h) % 4]
+                wrap(V(bk, 0, 80), V(jx, A + A * h, 2 * A + A * h), "W23")
+                cp(V("JU", 160 * s + 80 * h, 160 * s + 80 * h + 80), V(bk, 0, 80))
+            for h in range(2):
+                ga(V(jy, A + A * h, 2 * A + A * h), V(jx, 0, P), V("JU", 160 * s + 80 * h, 160 * s + 80 * h + 80), "a")
+            for c in range(4):
+                o = V(sy, A + 640 * c, A + 640 * c + 640)
+                c0 = c % 2 if rnd == 0 and s == 0 else c
+                gat(o, V(sx, 0, P), V("JU", 160 * s + 40 * c, 160 * s + 40 * c + 40), V("SC", 640 * c0, 640 * c0 + 640), add_)
+            for c in range(4 if s < 4 else 0):
+                cp(V("SC", 640 * c, 640 * c + 640), V(sy, A + 640 * c, A + 640 * c + 640), "sga" if c % 2 else "gsa")
+        JW = V("JB", 0, P)
+        ga(V("KT", KB, KB + NB), JW, V("L4U", 240, 256), "a")
+        for h in range(2):
+            ga(V("KT", 640 * h, 640 * h + 640), JW, V("L4U", 40 * h, 40 * h + 40))
+        wrap(V("P0", 0, 16), V("KT", KB, KB + NB), "W23")
+        atu = V("U", 980, 996)
+        ts(atu, V("P0", 0, 16), float(A), mn)
+        cp(V("K4", 240, 256), V("P0", 0, 16))
+        gat(V("EQ", 0, NB), V("KT", 0, KA), atu, V("LX", P + 3840, 2 * P), ALU.is_equal)
+        wrap(V("P1", 0, 16), V("EQ", 0, NB), "W23")
+        SF, RF, SX, RX, RP = ("%s%d" % (s, rnd) for s in ("SF", "RF", "SX", "RX", "RP"))
+        ts(V(SF, 0, 16), V("P1", 0, 16), 65.0, ALU.is_equal)
+        send(V(RF, 0, 16), V(SF, 0, 16), rnd)
+        ga(V(SX, 0, NB), V(XN, 0, KA), atu)
+        send(V(RX, 0, NB), V(SX, 0, NB), rnd)
+        if rnd == 0:
+            own = V("SP0", 0, NB)
+            ga(own, V("SB", 0, P), V("L4U", 240, 256))
+        else:
+            own = V("Q", 3840, P)
+            gat(own, V("SB", 0, P), V("LU", 240, 256), V("PH", 3840, P), add_)
+            ts(own, own, 15, band)
+        send(V(RP, 0, NB), own, rnd)
+        for h in range(2):
+            ga(V("KT", KA + A * h, KA + A * h + A), JW, V("L4U", 80 + 80 * h, 160 + 80 * h))
+        wrap(V("P2", 0, 80), V("KT", 0, A), "W23")
+        wrap(V("P3", 0, 80), V("KT", KA, KA + A), "W23")
+        wrap(V("P4B", 0, 80), V("KT", KA + A, KB), "W23")
+        tt(V("K4", 0, 80), V("P2", 0, 80), aq, sub)
+        tt(V("K4", 80, 160), V("P3", 0, 80), V("CC", 0, 80), add_)
+        tt(V("K4", 160, 240), V("P4B", 0, 80), V("CC", 80, 160), add_)
+        cp(V("L5U", 160, 256), V("K4", 160, 256))
+        aff(V("VR", 0, NB), V("KT", KB, KB + NB), bias=c_(7 + rnd))
+        cp(V("VR", NB, 2 * NB), V("KT", KB, KB + NB), "gav")
+        tt(V("AW", 0, 16), V("K4", 240, 256), V("KW", 0, 16), sub)
+        aff(V("AW", 16, 32), V("AW", 0, 16), bias=1024.0)
+        aff(V("AW", 32, 48), V("AW", 0, 16), bias=2816.0)
+        tt(V("AW", 48, 64), V("KW", 48, 64), pb, sub)
+        for j in range(4):
+            tt(V("AW", 64 + 16 * j, 80 + 16 * j), V("AW", 16 * j, 16 * j + 16), V(SF, 0, 16), mul)
+        dlt, d1, d2, k2 = w_(), w_(), w_(), w_()
+        tt(dlt, V("K4", 80, 160), V("K4", 0, 80), sub)
+        tt(d1, V(PL, 80, 160), V(PL, 0, 80), sub)
+        aff(k2, V("K4", 0, 80), bias=float(SS - 3840))
+        tt(d2, k2, V(PL, 80, 160), sub)
+        if rnd == 0:
+            ga(V("PH", 2 * A, 3 * A), V("SB", 0, P), V("L4U", 160, 240))
+        else:
+            for c in range(6):
+                o = V("Q", 640 * c, 640 * c + 640)
+                gat(o, V("SB", 0, P), V("LU", 40 * c, 40 * c + 40), V("PH", 640 * c, 640 * c + 640), add_)
+                ts(o, o, 15, band)
+                cp(V("JA", 640 * c, 640 * c + 640), o, "gv")
+            cp(V("JA", 3840, P), own, "gv")
+            for a in (2560, 3200):
+                ga(V("JB", a, a + 640), V("JA", 0, SS), V("P5U", a // 16, a // 16 + 40))
+                dma(("yp", a, a + 640, 1), V("JB", a, a + 640))
+        for j in range(2):
+            tt(V("BW", 16 * j, 16 * j + 16), V("AW", 64 + 16 * j, 80 + 16 * j), V(RF, 0, 16), mul)
+        tt(V("BW", 64, 96), V("BW", 0, 32), V("KW", 0, 32), add_)
+        cp(V("OU", 0, 32), V("BW", 64, 96))
+        sca(V(RHO, 0, 4608), V("OU", 0, 32), V("VR", 0, 512))
+        wrap(V("P0", 0, 80), V(RHO, 0, A), "WF%d" % rnd)
+        for j in range(2, 4):
+            tt(V("BW", 16 * j, 16 * j + 16), V("AW", 64 + 16 * j, 80 + 16 * j), V(RF, 0, 16), mul)
+        tt(V("BW", 96, 112), V("BW", 32, 48), V("KW", 32, 48), add_)
+        cp(V("OU", 32, 48), V("BW", 96, 112))
+        sca(V(XN, 0, 1536), V("OU", 32, 48), V(RX, 0, NB))
+        tt(V("P5", 240, 256), V("BW", 48, 64), pb, add_)
+        cp(V("P5U", 240, 256), V("P5", 240, 256))
+        sw = V("P0", 0, 80)
+        tt(px[0], sw, dlt, mul)
+        tt(V("L5", 0, 80), px[0], V("K4", 0, 80), add_)
+        cp(V("L5U", 0, 80), V("L5", 0, 80))
+        tt(V("L5", 80, 160), V("K4", 80, 160), px[0], sub)
+        cp(V("L5U", 80, 160), V("L5", 80, 160))
+        tt(px[1], sw, d1, mul)
+        tt(px[2], sw, d2, mul)
+        tt(V("P5", 0, 160), V("PX", 244, 404), V(PL, 0, 160), add_)
+        cp(V("P5U", 0, 160), V("P5", 0, 160))
+        RW = V(RHO, 0, P)
+        if rnd == 0:
+            for a in (0, 640):
+                cp(V("X5", a, a + 640), V("XB", a, a + 640), "gsva")
+            tt(V("SB", SS, SS + NB), own, V(RP, 0, NB), add_)
+            for h in range(2):
+                ga(V("LX", 640 * h, 640 * h + 640), RW, V("L5U", 40 * h, 40 * h + 40))
+            wrap(V("P1", 0, 80), V("LX", 0, A), "W23")
+            ts(cu, V("P1", 0, 80), 1279.0, mn)
+            cp(V("LW", 0, 80), V("P1", 0, 80))
+            ga(V("LX", 2 * A, P), RW, V("L5U", 160, 256))
+            ga(V("LX", A, 2 * A), RW, V("L5U", 80, 160))
+            wrap(V("P2", 0, 96), V("LX", 2 * A, P), "W23")
+            wrap(V("P3", 0, 80), V("LX", A, 2 * A), "W23")
+            cp(V("LW", 160, 256), V("P2", 0, 96), "a")
+            cp(V("LW", 80, 160), V("P3", 0, 80), "a")
+            cp(V("LU", 0, 256), V("LW", 0, 256))
+            SW = V("SB", 0, 4360)
+            ga(V("PH", A, 2 * A), SW, V("P5U", 80, 160))
+            ga(V("PH", 0, A), SW, V("P5U", 0, 80))
+            ga(V("PH", 3840, P), SW, V("P5U", 240, 256))
+        else:
+            dma(("yx", 0, A, 1), V(XN, 0, A))
+            qs = V("Q", SS, SS + NB)
+            tt(qs, own, V(RP, 0, NB), add_)
+            ts(qs, qs, 15, band)
+            cp(V("JA", SS, SS + NB), qs, "vg")
+            for a, b in ((3840, P), (0, 640), (640, A), (A, 1920), (1920, 2560)):
+                ga(V("JB", a, b), V("JA", 0, 4360), V("P5U", a // 16, b // 16))
+                dma(("yp", a, b, 1), V("JB", a, b))
+            for a, b in ((2560, 3328), (3328, P), (0, 768), (768, A), (A, 2048), (2048, 2560)):
+                ga(V("LX", a, b), RW, V("L5U", a // 16, b // 16))
+            for n, i in enumerate(list(range(10, 16)) + list(range(10))):
+                add("blk", "p", {"p": 0.02 + 256 * PCY}, [V("LX", 256 * i, 256 * i + 256), V("W23", 0, 144)], [V("P1", 0, 256)],
+                    i=i, start=n == 0, stop=n == 15)
+            cp(V("YL", 0, 256), V("P1", 0, 256), "a")
+            dma(("yl", 0, P, 1), V("YL", 0, 256))
+    return ops
+
+
+def graph(ops):
+    seen = {}
+    for n, o in enumerate(ops):
+        dep = set()
+        acc = [(r, False) for r in o["rd"]] + [(w, True) for w in o["wr"]]
+        for v, w in acc:
+            for m, a, b, pw in seen.get(v[0], []):
+                if ((w or pw) and a < v[2] and v[1] < b) or (v[0] in PSUM and ops[m]["engs"] != o["engs"]):
+                    dep.add(m)
+        for v, w in acc:
+            lst = seen.setdefault(v[0], [])
+            if w and v[3] == 1 and (v[0] not in PSUM or v[0] in ("PV", "PX")):
+                lst[:] = [x for x in lst if not (v[1] <= x[1] and x[2] <= v[2])]
+            lst.append((n, v[1], v[2], w))
+        dep.discard(n)
+        o["dep"] = sorted(dep)
+
+
+def schedule(cost, lat, pred, succ, pr, eng, back):
+    n = len(cost)
+    left = [len(x) for x in pred]
+    rdy = [lat[i].get(eng[i], 0.0) if back else 0.0 for i in range(n)]
+    bind = [-1] * n
+    ready = {e: [] for e in "vapgs"}
+    for i in range(n):
+        if left[i] == 0:
+            ready[eng[i]].append(i)
+    free = {e: 0.0 for e in "vapgs"}
+    prev = {e: -1 for e in "vapgs"}
+    out = []
+    end, last = 0.0, -1
+    for _ in range(n):
+        t0, e = min((max(free[x], min([rdy[i] for i in ready[x]])), x) for x in "vapgs" if ready[x])
+        i = max([(pr[j], j) for j in ready[e] if rdy[j] <= t0 + SLACK])[1]
+        ready[e].remove(i)
+        if free[e] > rdy[i]:
+            bind[i] = prev[e]
+        st = max(t0, rdy[i])
+        free[e] = st + cost[i][e]
+        prev[e] = i
+        fin = free[e] + (0.0 if back else lat[i].get(e, 0.0))
+        if fin > end:
+            end, last = fin, i
+        out.append((i, e, st, fin))
+        fin += LAT
+        for s in succ[i]:
+            f = fin + lat[s].get(eng[s], 0.0) if back else fin
+            if f > rdy[s]:
+                rdy[s] = f
+                bind[s] = i
+            left[s] -= 1
+            if left[s] == 0:
+                ready[eng[s]].append(s)
+    chain = []
+    while last >= 0:
+        chain.append(last)
+        last = bind[last]
+    return end, out, chain
+
+
+PLAN = {}
+
+
+def plan():
+    if not PLAN:
+        ops = build()
+        graph(ops)
+        n = len(ops)
+        pred = [o["dep"] for o in ops]
+        succ = [[] for _ in range(n)]
+        for i, o in enumerate(ops):
+            for d in o["dep"]:
+                succ[d].append(i)
+        cost, lat = [o["cost"] for o in ops], [o["lat"] for o in ops]
+        eng = [o["engs"][0] for o in ops]
+        pr = [0.0] * n
+        for i in range(n - 1, -1, -1):
+            pr[i] = cost[i][eng[i]] + lat[i].get(eng[i], 0.0) + LAT + max([pr[s] for s in succ[i]] + [0.0])
+        flex = [i for i in range(n) if len(ops[i]["engs"]) > 1]
+        cur = best = schedule(cost, lat, pred, succ, pr, eng, False)
+        rs = np.random.RandomState(1)
+        for t in range(TRIES):
+            e2 = list(eng)
+            fl = [i for i in cur[2] if len(ops[i]["engs"]) > 1]
+            u = rs.uniform()
+            if u < 0.7:
+                f = fl[int(rs.randint(len(fl)))] if u < 0.4 and fl else flex[int(rs.randint(len(flex)))]
+                other = ops[f]["engs"].replace(e2[f], "")
+                e2[f] = other[int(rs.randint(len(other)))]
+            p2 = [0.0] * n
+            for i, _e, _s, fin in cur[1]:
+                p2[i] = fin
+            for i in rs.randint(n, size=int(rs.randint(6))):
+                p2[int(i)] += float(rs.normal()) * 1.5
+            for i, _e, _s, fin in schedule(cost, lat, succ, pred, p2, e2, True)[1]:
+                p2[i] = fin
+            s = schedule(cost, lat, pred, succ, p2, e2, False)
+            if s[0] <= cur[0] + 0.5 * (1.0 - t / TRIES) * rs.uniform():
+                cur, eng = s, e2
+                if s[0] < best[0]:
+                    best = s
+        PLAN["ops"], PLAN["end"], PLAN["order"], PLAN["ch"] = ops, best[0], best[1], best[2]
+    return PLAN["ops"], PLAN["order"]
+
+
+def rank_program(g, core, T, topo):
+    rank = T.rank_of(core)
+    if rank is None:
+        return
+    ops, order = plan()
+    Q = {"v": g.vector, "a": g.scalar, "p": g.tensor, "g": g, "s": g.sync}
+    CS = {"v": "cv", "a": "ca", "p": "cp", "g": "cg"}
+
+    def ap(v):
+        if not isinstance(v, tuple):
+            return v
+        if v[0] == "yl":
+            return T.yl[:]
+        return T[v[0]][:, v[1]:v[2]:v[3]] if v[3] != 1 else T[v[0]][:, v[1]:v[2]]
+
+    count = {"cv": 0, "ca": 0, "cp": 0, "cg": 0}
+    total = {}
+    known = {e: {} for e in Q}
+    done = {}
+    nd = 0
+    for i, e, _st, _fin in order:
+        o = ops[i]
+        kind = o["kind"]
+        k = {n: ap(v) for n, v in o["k"].items()}
+        q = Q[e]
+        kn = known[e]
+        need = {}
+        for d in o["dep"]:
+            if kind == "blk" and ops[d]["kind"] == "blk":
+                continue
+            sem, val, snap = done[d]
+            if need.get(sem, (0, None))[0] < val:
+                need[sem] = (val, snap)
+        for sem in sorted(need, key=lambda s: -len(need[s][1])):
+            val, snap = need[sem]
+            if kn.get(sem, 0) < val:
+                q.wait_ge(T.sem[sem], val)
+                kn[sem] = val
+                for s2, v2 in snap.items():
+                    if kn.get(s2, 0) < v2:
+                        kn[s2] = v2
+        if e == "s" or "dma" in k:
+            sem = "d%d" % nd
+            nd += 1
+            if "rows" in k:
+                for r0 in (2, 3):
+                    q.dma_start(T.MIX[r0:128:16, 0:A], T.LX[r0:128:16, 0:A]).then_inc(T.sem[sem], 16)
+            else:
+                q.dma_start(k["o"], k["i"]).then_inc(T.sem[sem], 16)
+            total[sem] = 32 if "rows" in k else 16
+            done[i] = (sem, total[sem], dict(kn))
+            continue
+        if kind == "send":
+            peer = T.cores[rank ^ XM[k["rnd"]]]
+            rid, pid, _se = topo.addr(peer)
+            g.remote_dma(k["o"], k["i"], T.sem[k["sem"]], T.sem.sent, pid, rid, topo.mask(core, peer))
+            total["sent"] = total.get("sent", 0) + len(topo.engines(core, peer))
+            total[k["sem"]] = len(topo.engines(peer, core))
+            done[i] = (k["sem"], total[k["sem"]], {})
+            continue
+        if kind in ("ga", "gat", "sca"):
+            ind = k["w"].indirect(k["l"])
+        if kind == "ts":
+            if k["op1"] is None:
+                r = q.tensor_scalar(k["o"], k["i"], k["s1"], None, k["op0"])
+            else:
+                r = q.tensor_scalar(k["o"], k["i"], k["s1"], k["s2"], k["op0"], k["op1"])
+        elif kind == "tt":
+            r = q.tensor_tensor(k["o"], k["a"], k["b"], k["op"])
+        elif kind == "cp":
+            if e == "g":
+                r = q.affine_select(k["o"], k["i"], [[0, width(o["k"]["o"])]], ALU.is_ge, 0.0, 0, 0)
+            else:
+                r = q.tensor_copy(k["o"], k["i"]) if e == "v" else q.activation(k["o"], k["i"], ACT.Copy)
+        elif kind == "aff":
+            if e == "a":
+                r = q.activation(k["o"], k["i"], ACT.Identity, bias=k["bias"], scale=k["scale"])
+            elif o["k"]["scale"] == 1.0:
+                r = q.tensor_scalar(k["o"], k["i"], k["bias"], None, ALU.add)
+            else:
+                r = q.tensor_scalar(k["o"], k["i"], k["scale"], k["bias"], ALU.mult, ALU.add)
+        elif kind == "abs":
+            r = q.activation(k["o"], k["i"], ACT.Abs, bias=k["bias"])
+        elif kind == "tri":
+            r = q.affine_select(k["o"], k["i"], [[-1, 128]], ALU.is_ge, 0.0, 0, 1)
+        elif kind == "ga":
+            if e == "a":
+                r = q.activation(k["o"], ind, ACT.Copy) if k["scale"] is None else q.activation(k["o"], ind, ACT.Identity, scale=k["scale"])
+            else:
+                r = q.tensor_copy(k["o"], ind) if k["scale"] is None else q.tensor_scalar(k["o"], ind, k["scale"], None, ALU.mult)
+        elif kind == "gat":
+            r = q.tensor_tensor(k["o"], ind, k["b"], k["op"])
+        elif kind == "sca":
+            r = q.tensor_copy(ind, k["i"])
+        elif kind == "wrap":
+            t = o["k"]["t"]
+            for j in range(16):
+                r = q.matmul(k["o"], T[k["m"]][:, 15 - j:143 - j], T[t[0]][:, t[1] + j:t[2]:16], j == 0, j == 15)
+        elif kind == "blk":
+            j = k["i"]
+            r = q.matmul(T.P1[:, 0:256], T.W23[:, 15 - j:143 - j], T.LX[:, 256 * j:256 * j + 256], k["start"], k["stop"])
+        elif kind == "mm":
+            for j, (oo, l, rr) in enumerate(k["items"]):
+                r = q.matmul(ap(oo), ap(l), ap(rr), j == 0 or not k["acc"], j == len(k["items"]) - 1 or not k["acc"])
+        elif kind == "scan":
+            r = q.tensor_tensor_scan(k["o"], k["a"], k["b"], 0.0, ALU.mult, ALU.add)
+        elif SCRATCH[o["k"]["o"][0]][2] == I32:
+            r = q.iota(k["o"], k["pat"], k["base"], k["cm"])
+        else:
+            r = q.iota(k["o"], k["pat"], k["base"], k["cm"], allow_small_or_imprecise_dtypes=True)
+        sem = CS[e]
+        r.then_inc(T.sem[sem], 1)
+        count[sem] += 1
+        done[i] = (sem, count[sem], dict(kn))
+    total.update(count)
+    for sem in sorted(total):
+        if total[sem] and known["g"].get(sem, 0) < total[sem]:
+            g.wait_ge(T.sem[sem], total[sem])

@@ -1,33 +1,42 @@
+import math
 import numpy as np
 from concourse.mybir import AluOpType as ALU, ActivationFunctionType as ACT
 
 A, NB, P = 1280, 256, 4096
 XM = (1, 2)
-Z = 4096
-SS = 4104
+PO = 2816
+FB, UB, NT = 1600, 2881, 3536
 KA, KB = 1296, 3856
+SS, QS = 6656, 5376
+BIG = 8192.0
+SP = 640
 
 BF, F32, I32, U16 = "bfloat16", "float32", "int32", "uint16"
+WN = ("W23", "WP", "WD1", "WD2", "WD3", "WD4", "WN", "WV", "WF")
+SIG = ({1: 1}, {1: 1, 2: 44}, {0: -1, 1: 1, 3: -20}, {0: -1, 2: 1, 3: -40}, {0: -1, 1: 1, 3: 20, 4: -1, 5: 1, 7: 40},
+       {0: -1, 2: 1, 3: 20, 4: -1, 6: 1, 7: 40}, {3: 1, 7: 1}, {0: 1, 3: -64}, {4: 1})
+MN = ("MU", "M45", "MB", "MV", "M89", "MC", "ME", "MO")
+SHF = ((0, 0), (4, -999), (-999, -999), (2, -2), (8, -999), (12, -999), (10, -999), (-999, 8))
 SCRATCH = {}
 for _d, _l in (
-        (I32, "LK:256 THI:2 Q:4360 RP1:256 PI:4 RI:82 HF:82 OD:82"),
-        (BF, "THB:2 LX:8192 JA:4360 JB:4096 KT:4112 RHO0:4608 RHO1:4608 ST:3200 XA:3216 XB:3216 XC:1536 X5:1280 DB:1280 DM:1280 MIX:1280 "
-             "TP:1280 TM:1280 TM2:1280 TT:336 DU:320 X2:320 S1:320 S2:320 EQ:256 VR:512 SX0:256 SX1:256 RX0:256 RX1:256 "
-             "W23:144 W01:144 WD:144 WS:144 WF0:144 WF1:144 W45:144 W67:144 WU:144 ONES:128 TRI:128 DG1:128 DG2:128 DG3:128 FL:164"),
-        (F32, "TH:2 SA:4096 SB:4360 SC:2560 PH:4104 YL:256 SP0:256 RP0:256 SF0:16 SF1:16 RF0:16 RF1:16 R:144 C:20 E:16 HI2:64 HI0:64 "
-              "PR:256 PW:256 CW:880 KW:64 MA:128 MB:128 MC:128 D0:164 SN:164 RK:164 LW:256 L4:256 K4:256 P4:256 L5:256 P5:256 "
-              "W:3040 JAW:160 CL:160 CC:160 AW:128 BW:128"),
-        (U16, "LU:256 L4U:256 L5U:256 P5U:256 JU:800 U:1040 OU:64")):
+        (I32, "LK:256 THI:2 Q:4352 RP1:256 PI:6"),
+        (BF, "THB:2 LX:10752 JA:5632 JB:4096 KT:4112 RHO:5632 ST:3536 TT:3536 VT:320 XA:2240 XB:2240 DA:1296 "
+             "DM:1280 MIX:1280 TP:1280 TM:1280 X1:320 S1:320 EQ:256 VR:256 SX0:256 SX1:256 RX0:256 RX1:256 WS:144 WM:144 "
+             "ONES:128 TRI:128 TR0:128 I1:128 IA:128 IP:128 NI:128 TQ:128 FL:164 HB:400 " + " ".join(w + ":144" for w in WN) + " " + " ".join(m + ":128" for m in MN)),
+        (F32, "TH:10 SA:4096 SB:4096 SF:6912 PH:4104 SP0:256 RP0:256 SF0:32 SF1:32 RF0:32 RF1:32 R:144 C:24 E:16 HI2:64 "
+              "PW:256 KW:96 I32:128 MB2:128 D0:164 SN:164 RK:164 LW:256 PL:160 K4:160 W:1280 CL:160 TW:160 AW:96 BW:128 "
+              "CW:9 CT:8 SC:2560"),
+        (U16, "LU:256 F4U:256 L5U:256 P5U:256 JU:800 U:800 OU:64")):
     for _x in _l.split():
         SCRATCH[_x.split(":")[0]] = ("sbuf", [128, int(_x.split(":")[1])], _d)
-PSUM = ("P0", "P1", "P2", "P3", "P4B", "P5B", "PV", "PX")
+PSUM = ("P0", "P1", "P2", "P3", "P4B", "P5B", "P6B", "PX")
 for _n in PSUM:
     SCRATCH[_n] = ("psum", [128, 512], F32)
 SEMAPHORES = ["cv", "ca", "cp", "cg", "sent"] + ["d%d" % i for i in range(110)] + ["arr%d" % i for i in range(6)]
 
 CY, PCY = 0.83e-3, 0.83e-3
-GA, SCA, FIX, BW, LAT = 1.56, 3.8, 0.05, 190e3, 0.06
-TRIES, SLACK = 5000, 0.12
+GA, SCA, FIX, BW, LAT, DL, RL = 1.56, 3.8, 0.05, 190e3, 0.06, 2.0, 2.5
+STEPS, HEAT, TRIES, SLACK, SEED = 350000, 0.3, 1000, 0.12, 1
 
 
 def V(n, a, b, s=1):
@@ -63,7 +72,7 @@ def build():
         add("tt", "v", {"v": FIX + max(64, c) * CY}, [a, b], [o], o=o, a=a, b=b, op=op)
 
     def cp(o, i, engs="v"):
-        add("cp", engs, plain(o, i), [i], [o], lat={"s": 2.0}, o=o, i=i)
+        add("cp", engs, plain(o, i), [i], [o], lat={"s": DL}, o=o, i=i)
 
     def aff(o, i, bias=0.0, scale=1.0, engs="av"):
         add("aff", engs, plain(o, i), [i, bias, scale], [o], o=o, i=i, bias=bias, scale=scale)
@@ -71,9 +80,12 @@ def build():
     def ab(o, i, bias=0.0):
         add("abs", "a", plain(o, i), [i, bias], [o], o=o, i=i, bias=bias)
 
-    def ga(o, w, l, engs="av", scale=None):
+    def relu(o, i, bias):
+        add("relu", "av", plain(o, i), [i, bias], [o], o=o, i=i, bias=bias, scale=1.0)
+
+    def ga(o, w, l, engs="av"):
         n = width(o)
-        add("ga", engs, {"v": 0.05 + n * GA * CY, "a": 0.065 + n * GA * CY}, [w, l], [o], o=o, w=w, l=l, scale=scale)
+        add("ga", engs, {"v": 0.05 + n * GA * CY, "a": 0.065 + n * GA * CY}, [w, l], [o], o=o, w=w, l=l, scale=None)
 
     def gat(o, w, l, b, op):
         add("gat", "v", {"v": 0.05 + width(o) * GA * CY}, [w, l, b], [o], o=o, w=w, l=l, b=b, op=op)
@@ -81,28 +93,38 @@ def build():
     def sca(w, l, i):
         add("sca", "v", {"v": 0.05 + width(i) * SCA * CY}, [l, i], [w], w=w, l=l, i=i)
 
-    def wrap(o, t, m):
-        add("wrap", "p", {"p": 0.05 + 16 * max(64, width(o)) * PCY}, [t, V(m, 0, 144)], [o], o=o, t=t, m=m)
+    def wrap(o, t, m, extra=(), start=True, stop=True, prev=None):
+        c = 16 * max(64, width(o)) + sum(max(64, width(o)) * (1 if narrow(r) else 4) for _l, r in extra)
+        add("wrap", "p", {"p": 0.05 + c * PCY}, [t, V(m, 0, 144)] + [x for y in extra for x in y], [o],
+            o=o, t=t, m=m, extra=list(extra), start=start, stop=stop, prev=prev)
+        return len(ops) - 1
 
     def mm(items, acc):
         add("mm", "p", {"p": 0.05 + sum(max(64, width(x[0])) for x in items) * PCY}, [x[1] for x in items] + [x[2] for x in items],
             [x[0] for x in items], items=items, acc=acc)
 
+    def scan(o, a, b, init):
+        add("scan", "v", plain(o, o), [a, b], [o], o=o, a=a, b=b, init=init)
+
     def io(o, pat, base, cm):
         add("iota", "g", {"g": 0.13 + 2 * width(o) * CY}, [], [o], o=o, pat=pat, base=base, cm=cm)
 
-    def zero(o):
-        io(o, [[0, width(o)]], 0, 0)
+    def zero(o, engs="g"):
+        c = plain(o, o)
+        add("ms", engs, {"g": 0.13 + 2 * width(o) * CY, "v": c["v"]}, [], [o], o=o, c=0.0)
 
     def dma(o, i, eng="s"):
         v = o if o[0] in SCRATCH else i
-        add("cp", eng, {"s": plain(v, v)["s"], "a": 0.06}, [i], [o], lat={"s": 2.0, "a": 2.0}, o=o, i=i, dma=True)
+        add("cp", eng, {"s": plain(v, v)["s"], "a": 0.06}, [i], [o], lat={"s": DL, "a": DL}, o=o, i=i, dma=True)
+
+    def rows(lst):
+        add("cp", "s", {"s": 0.12 * len(lst)}, [x[3] for x in lst], [x[1] for x in lst], lat={"s": DL}, rows=lst)
 
     nr = [0]
 
     def send(o, i, rnd):
         by = width(i) * (2 if narrow(i) else 4) * 128
-        add("send", "g", {"g": 0.3}, [i], [o], lat={"g": 2.5 + by / 80e3}, o=o, i=i, rnd=rnd, sem="arr%d" % nr[0])
+        add("send", "g", {"g": 0.3}, [i], [o], lat={"g": RL + by / 80e3}, o=o, i=i, rnd=rnd, sem="arr%d" % nr[0])
         nr[0] += 1
 
     def c_(j):
@@ -114,6 +136,9 @@ def build():
     def sub_(v, a, b):
         return V(v[0], v[1] + a, v[1] + b)
 
+    def m_(n):
+        return V(n, 0, 128)
+
     add_, sub, mul, mx, mn, band = ALU.add, ALU.subtract, ALU.mult, ALU.max, ALU.min, ALU.bitwise_and
     IOT = V("LX", P, 2 * P)
     X0 = V("Q", 0, A)
@@ -123,87 +148,132 @@ def build():
     dma(V("THI", 0, 2), ("th", 0, 2, 1), "a")
     io(V("PI", 0, 1), [[0, 1]], 0, 1)
     io(V("R", 0, 144), [[1, 144]], 0, 0)
-    io(V("PR", 0, 256), [[16, 256]], 0, 1)
-    ts(V("PI", 1, 2), V("PI", 0, 1), 15, band)
-    ts(V("PI", 2, 3), V("PI", 0, 1), 112, band)
-    cp(V("C", 0, 3), V("PI", 0, 3))
+    io(V("PW", 0, 256), [[16, 256]], 0, 1)
+    for j, b in ((1, 15), (2, 112), (3, 14), (4, 1)):
+        ts(V("PI", j, j + 1), V("PI", 0, 1), b, band)
+    cp(V("C", 0, 5), V("PI", 0, 5))
     ts(V("E", 0, 16), V("R", 0, 16), c_(1), ALU.is_equal)
     ts(V("HI2", 0, 64), V("R", 0, 64), e_(2), mul)
     ts(V("LX", P, P + 64), V("R", 0, 64), e_(3), mul)
     n = 64
-    while n < 1024:
-        aff(V("LX", P + n, P + 2 * n), V("LX", P, P + n), bias=V("HI2", n // 64, n // 64 + 1), engs="v")
-        n *= 2
-    for j in (1, 2, 3):
-        aff(V("LX", P + 1024 * j, P + 1024 * (j + 1)), V("LX", P, P + 1024), bias=V("HI2", 16 * j, 16 * j + 1), engs="va")
-    ts(c_(10), e_(0), e_(4), add_, e_(6), add_)
-    ts(c_(11), e_(1), e_(5), add_, e_(7), add_)
-    aff(V("HI0", 0, 64), V("R", 0, 64), scale=c_(10), engs="a")
-    aff(V("MIX", 0, 64), V("R", 0, 64), scale=c_(11), engs="a")
-    n = 64
     while n < A:
         m = min(n, A - n)
-        aff(V("MIX", n, n + m), V("MIX", 0, m), bias=V("HI0", n // 64, n // 64 + 1), engs="a")
+        aff(V("LX", P + n, P + n + m), V("LX", P, P + m), bias=V("HI2", n // 64, n // 64 + 1), engs="v")
         n *= 2
-    ts(c_(3), c_(2), 15.0, add_)
-    for c, h in ((4, 2), (5, 0), (15, 4), (16, 6)):
-        aff(c_(c), e_(h), scale=64.0, bias=e_(h + 1))
-    aff(c_(6), c_(5), scale=-1.0, bias=c_(4))
-    aff(c_(17), c_(15), bias=c_(16))
-    aff(c_(7), e_(2), scale=20.0, bias=e_(8))
-    aff(c_(8), e_(2), scale=20.0, bias=e_(9))
-    ts(c_(12), c_(1), 4.0, ALU.is_lt)
-    aff(c_(13), e_(4), bias=e_(5))
-    aff(c_(14), e_(6), bias=e_(7))
+    aff(c_(5), e_(2), scale=20.0, bias=e_(4))
+    aff(c_(6), e_(2), scale=40.0, bias=e_(4))
+    aff(V("LX", P + A, P + 2 * A), V("LX", P, P + A), bias=c_(5), engs="va")
+    aff(V("LX", P + 2 * A, P + 3 * A), V("LX", P, P + A), bias=c_(6), engs="va")
+    aff(V("LX", P + 3 * A, 2 * P), V("LX", P, P + NB), bias=V("HI2", 60, 61), engs="va")
+    zero(V("MIX", 0, A), "gv")
+    rows([(0, V("MIX", 0, A), 2, V("LX", P, P + A)), (1, V("MIX", 0, A), 3, V("LX", P, P + A)), (6, V("MIX", 0, A), 4, V("LX", P + A, P + 2 * A))])
+    zero(V("W", 0, 136))
+    for j, sg in enumerate(SIG):
+        ks = sorted(sg)
+        while ks:
+            if len(ks) > 1 and ks[1] == ks[0] + 1:
+                io(V("W", 8 * j + ks[0], 8 * j + ks[0] + 2), [[sg[ks[1]] - sg[ks[0]], 2]], sg[ks[0]], 0)
+                ks = ks[2:]
+            else:
+                io(V("W", 8 * j + ks[0], 8 * j + ks[0] + 1), [[0, 1]], sg[ks[0]], 0)
+                ks = ks[1:]
+    io(V("W", 75, 136, 8), [[0, 8]], -6, 0)
+    for j, (s0, s1) in enumerate(SHF):
+        if j:
+            io(V("W", 72 + 8 * j, 74 + 8 * j), [[s1 - s0, 2]], s0, 0)
+    HR, HO, HD = V("W", 160, 296), V("W", 320, 456), V("W", 480, 616)
+    io(HR, [[0, 17], [2, 8]], 0, 0)
+    ts(HO, HR, c_(3), ALU.is_equal)
+    ts(HD, HR, 0.0, ALU.is_gt)
+    tt(HR, HO, V("W", 0, 136), mul)
+    scan(V("W", 640, 776), HD, HR, 0.0)
+    aff(c_(7), c_(4), scale=-63.0, bias=64.0)
+    aff(V("CW", 0, 9), V("W", 647, 712, 8), scale=c_(7))
+    aff(V("CT", 0, 8), V("W", 719, 776, 8), bias=c_(0))
+    aff(V("CW", 6, 9, 2), V("CW", 6, 9, 2), scale=1.0 / 64)
+    aff(c_(8), c_(2), bias=15.0)
     WS = V("WS", 0, 144)
-    ts(WS, V("R", 0, 144), c_(3), ALU.is_equal)
-    for m, cl in (("W23", c_(4)), ("W01", c_(5)), ("WD", c_(6)), ("WF0", e_(8)), ("WF1", e_(9)), ("W45", c_(15)), ("W67", c_(16)), ("WU", c_(17))):
-        aff(V(m, 0, 144), WS, scale=cl)
-    R8, MA, MB, MC = V("R", 0, 128), V("MA", 0, 128), V("MB", 0, 128), V("MC", 0, 128)
-    ONES, TRI, FL = V("ONES", 0, 128), V("TRI", 0, 128), V("FL", 0, 164)
-    ts(MA, R8, c_(0), ALU.is_equal)
-    for j in (1, 2, 3):
-        aff(V("DG%d" % j, 0, 128), MA, scale=c_(11 + j))
-    aff(c_(18), c_(2), scale=-1.0, bias=-7.5)
-    ab(MB, R8, c_(18))
-    ts(ONES, MB, 8.0, ALU.is_lt)
-    aff(MC, ONES, scale=-1.0)
-    add("tri", "g", plain(TRI, MC), [MC], [TRI], o=TRI, i=MC)
-    ts(V("PW", 0, 256), V("PR", 0, 256), c_(2), sub)
-    col, col2A = V("PW", 0, 80), V("PW", 160, 240)
-    B1, B2, colcol = V("CW", 0, 80), V("CW", 80, 160), V("CW", 160, 320)
-    aff(V("CW", 0, 160), V("PW", 80, 240), bias=4096.0)
-    cp(V("CW", 160, 240), col, "avg")
-    cp(V("CW", 240, 320), col, "avg")
-    cm2A, cmA, cm1296, c2m = V("CW", 320, 400), V("CW", 400, 480), V("CW", 480, 560), V("CW", 800, 880)
-    aff(cm2A, col, bias=-2.0 * A)
-    aff(cmA, col, bias=-1.0 * A)
-    aff(cm1296, col, bias=-1296.0)
-    aff(c2m, col, bias=-2.0 * A, scale=2.0)
-    aff(V("CW", 560, 800), V("PW", 0, 240), bias=float(Z), scale=-1.0)
-    for j, b in enumerate((4096.0, 4352.0, 1280.0, float(SS))):
+    ts(WS, V("R", 0, 144), c_(8), ALU.is_equal)
+    for j, m in enumerate(WN):
+        aff(V(m, 0, 144), WS, scale=V("CW", j, j + 1), engs="va")
+    aff(V("WM", 0, 144), V("W23", 0, 144), scale=512.0, engs="va")
+    R8 = V("R", 0, 128)
+    ONES, TRI, FL = m_("ONES"), m_("TRI"), V("FL", 0, 164)
+    ts(m_("I32"), R8, c_(0), ALU.is_equal)
+    for m, s in (("I1", 1.0), ("IA", float(A)), ("IP", float(P)), ("NI", -512.0)):
+        aff(m_(m), m_("I32"), scale=s)
+    aff(c_(9), c_(2), scale=-1.0, bias=-7.5)
+    ab(m_("MB2"), R8, c_(9))
+    ts(ONES, m_("MB2"), 8.0, ALU.is_lt)
+    ts(m_("TQ"), m_("MB2"), 8.0, ALU.is_lt, -1.0, mul)
+    add("tri", "g", plain(TRI, TRI), [m_("TQ")], [m_("TR0")], o=m_("TR0"), i=m_("TQ"))
+    tt(TRI, m_("TR0"), m_("IP"), add_)
+    io(m_("MB2"), [[0, 8], [-1, 16]], 0, 0)
+    ts(m_("MB2"), m_("MB2"), e_(6), mul)
+    tt(m_("TQ"), m_("MB2"), R8, add_)
+    aff(c_(10), e_(6), scale=127.0, bias=1.0)
+    for j, m in enumerate(MN):
+        ts(m_(m), m_("TQ"), V("CT", j, j + 1), ALU.is_equal, c_(10), mul)
+    aff(c_(11), e_(6), bias=-384.0)
+    aff(c_(12), e_(6), bias=-256.0)
+    aff(c_(13), e_(14), bias=-384.0)
+    aff(c_(14), c_(5), bias=e_(8))
+    ts(V("PW", 0, 256), V("PW", 0, 256), c_(2), sub)
+    col, colA = V("PW", 0, 80), V("HB", 0, 80)
+    io(colA, [[16, 80]], 0, 0)
+    for j, b in ((0, 4096.0), (2, 1280.0)):
         aff(V("KW", 16 * j, 16 * j + 16), V("PW", 0, 16), bias=b)
+    aff(V("KW", 64, 84), V("PW", 0, 20), bias=float(A - P))
     zero(FL)
-    io(V("FL", 0, 1), [[0, 1]], 80, 0)
-    io(V("FL", 82, 83), [[0, 1]], 160, 0)
+    io(V("FL", 82, 83), [[0, 1]], -76, 0)
     io(V("D0", 0, 164), [[0, 164]], 1, 0)
     zero(V("D0", 82, 83))
     cp(V("THB", 0, 2), V("THI", 0, 2))
     mm([(V("P5B", 0, 2), ONES, V("THB", 0, 2))], False)
-    cp(V("TH", 0, 2), V("P5B", 0, 2), "a")
-    for v in (V("XA", 2560, 2576), V("ST", 0, 1600), V("ST", 1600, 3200), V("LX", 3840, P), V("SA", 0, A), V("SA", 3840, P), V("SB", 0, A),
-              V("SB", 3840, SS), V("KT", A, KA), V("PH", P, SS), V("JA", P, SS), V("XB", A, 1536), V("XB", 2560, 2576),
-              V("XC", A, 1536), V("TT", 320, 336)):
+    aff(c_(16), c_(1), scale=-512.0, bias=0.5)
+    aff(c_(17), c_(1), scale=-512.0, bias=-120.0)
+    aff(V("TH", 0, 2), V("P5B", 0, 2), scale=-0.5, bias=c_(16), engs="a")
+    aff(V("TH", 2, 4), V("P5B", 0, 2), scale=0.5, bias=-0.25, engs="a")
+    aff(V("TH", 4, 6), V("P5B", 0, 2), scale=-0.5, bias=c_(17), engs="a")
+    aff(V("TH", 6, 8), V("P5B", 0, 2), scale=-0.5, bias=120.25, engs="a")
+    for v in (V("JA", P, QS), V("XA", A, FB), V("DA", A, KA), V("SA", 0, A), V("KT", A, KA), V("PH", P, P + 8)):
         zero(v)
+
+    def zc(n, a, b, engs="sg"):
+        while a < b:
+            m = min(A, b - a)
+            cp(V(n, a, a + m), V("JA", P, P + m) if SCRATCH[n][2] == BF else V("SA", 0, m), engs)
+            ops[-1]["rd"].append(V("Q", 0, 8))
+            a += m
+
+    zc("TT", FB + 640, UB + 7)
+    zc("TT", UB + 319, NT)
+    zc("XB", A, FB)
+    zc("SA", 3840, P)
+    zc("SB", 0, A)
+    zc("SB", 3840, P)
+    zc("SF", 0, P)
+    zc("SF", SS, SS + NB)
 
     cu = V("U", 0, 80)
     cp(V("LU", 0, 256), V("LK", 0, 256))
     ts(cu, V("LK", 0, 80), 1279, mn)
-    cp(V("LW", 0, 256), V("LK", 0, 256), "vg")
-    for j in range(6):
-        ga(V("LX", 640 * j, 640 * (j + 1)), IOT, V("LU", 40 * j, 40 * j + 40))
+    cp(V("LW", 0, 80), V("LK", 0, 80), "vg")
+    for a, b in ((0, 640), (640, A), (A, 1920), (1920, 2560), (2560, 3200), (3200, P)):
+        ga(V("LX", a, b), IOT, V("LU", a // 16, b // 16))
     for a in (0, 640):
         cp(V("XA", a, a + 640), V("Q", a, a + 640), "vg")
+
+    def primed(rnd):
+        wrap(V("P3", 0, 96), V("LX", 2 * A, P), "WP")
+        wrap(V("P4B", 0, 80), V("LX", A, 2 * A), "WP")
+        cp(V("LW", 160, 256), V("P3", 0, 96), "av")
+        cp(V("LW", 80, 160), V("P4B", 0, 80), "av")
+        cp(V("F4U", 240, 256), V("LW", 240, 256))
+        if rnd:
+            wrap(V("P5B", 0, 80), V("LX", 0, A), "WP")
+            cp(V("LU", 0, 80), V("P5B", 0, 80))
+            cp(V("LU", 80, 256), V("LW", 80, 256))
 
     wi = [0]
 
@@ -213,305 +283,252 @@ def build():
 
     for rnd in range(2):
         wi[0] = 0
-        X, XN = (("XA", "XB"), ("XB", "XC"))[rnd]
-        RHO = "RHO%d" % rnd
+        X, XN = (("XA", "XB"), ("XB", "XA"))[rnd]
+        RHO = "RHO"
         q, free, cand = V("LW", 0, 80), V("FL", 1, 81), V("FL", 83, 163)
-        ann, pf, dbl, act, spec = (V("PV", 80 * j, 80 * j + 80) for j in range(5))
-        px = [V("PX", 164 + 80 * j, 244 + 80 * j) for j in range(4)]
-        xw, xi = (X0, V("XA", 0, A)) if rnd == 0 else (V("XB", 0, A), V("X5", 0, A))
+        nf, ann = V("HB", 80, 160), V("HB", 160, 240)
+        px = [V("PX", 80 * j, 80 * j + 80) for j in range(4)]
+        xw = X0 if rnd == 0 else V("XB", 0, A)
+        zc("ST", FB if rnd else 0, NT)
+        zc("TT", 0, FB)
+        qa, hg, qm, y1, y2, e1, z, o2 = (w_() for _ in range(8))
+        for h in range(2):
+            ga(V("TP", 640 * h, 640 * h + 640), V("LX", 0, A), sub_(cu, 40 * h, 40 * h + 40))
+        tt(qa, q, col, sub)
+        ts(free, qa, 0.0, ALU.is_equal)
+        ts(nf, q, float(A), ALU.is_ge, BIG, mul)
+        ts(hg, qa, 0.0, ALU.is_gt, V("TH", 6 + rnd, 7 + rnd), mul)
+        aff(qm, qa, bias=-4096.0)
+        w0 = wrap(V("P0", 0, 80), V("TP", 0, A), "WM", [(m_("NI"), colA), (m_("NI"), free), (m_("NI"), nf)], stop=False)
         for h in range(2):
             a, b = 640 * h, 640 * h + 640
-            gat(V("DB", a, b), xw, sub_(cu, 40 * h, 40 * h + 40), sub_(xi, a, b), sub)
-            ab(V(X, A + a, A + b), V("DB", a, b))
-            ga(V("TP", a, b), V("LX", 0, A), sub_(cu, 40 * h, 40 * h + 40))
-        wrap(V("P0", 0, 80), V("TP", 0, A), "W23")
-        wrap(V("P1", 0, 80), V(X, A, 2 * A), "WS")
-        qa, gt, colx, e1, pair, isV, fus = (w_() for _ in range(7))
-        tt(free, q, col, ALU.is_equal)
-        tt(qa, q, col, sub)
-        ts(gt, qa, 0.0, ALU.is_gt)
-        ts(px[0], q, float(A), ALU.is_ge, 8192.0, mul)
-        tt(colx, px[0], col, add_)
-        tt(px[1], V("P0", 0, 80), colx, ALU.is_equal)
-        tt(pair, px[1], free, sub)
-        ts(px[0], V("P1", 0, 80), V("TH", rnd, rnd + 1), ALU.is_lt)
-        tt(ann, px[0], pair, mul)
-        tt(pf, ann, pair, ALU.is_lt)
-        tt(cand, pf, gt, mul)
+            gat(V("DM", a, b), xw, sub_(cu, 40 * h, 40 * h + 40), V("XA", a, b), sub)
+            ab(V("DA", a, b), V("DM", a, b))
+        wrap(V("P0", 0, 80), V("DA", 0, A), "WS", start=False, prev=w0)
+        ab(y2, V("P0", 0, 80), V("TH", 4 + rnd, 5 + rnd))
+        ab(y1, V("P0", 0, 80), V("TH", rnd, rnd + 1))
+        tt(cand, y2, hg, ALU.is_lt)
+        ts(ann, y1, V("TH", 2 + rnd, 3 + rnd), ALU.is_lt)
         mm([(V("P2", 0, 164), ONES, FL), (V("P2", 200, 364), TRI, FL)], False)
-        add("scan", "v", {"v": FIX + 164 * CY}, [V("D0", 0, 164), V("P2", 0, 164)], [V("SN", 0, 164)], o=V("SN", 0, 164), a=V("D0", 0, 164), b=V("P2", 0, 164))
+        scan(V("SN", 0, 164), V("D0", 0, 164), V("P2", 0, 164), float(FB - 4097))
         tt(V("RK", 0, 164), V("P2", 200, 364), V("SN", 0, 164), add_)
         valF = V("RK", 1, 81)
-        offu = V("U", 160, 240)
-        tt(V("PX", 0, 164), V("RK", 0, 164), FL, mul)
-        o1, o2 = w_(), w_()
-        tt(o1, V("PX", 1, 81), col, mx)
-        tt(o2, V("PX", 83, 163), o1, mx)
+        offu = V("U", 80, 160)
+        tt(px[0], valF, col, mx)
+        tt(o2, px[0], V("RK", 83, 163), mx)
         cp(offu, o2)
-        add("cp", "s", {"s": 0.25}, [V("LX", 0, A)], [V("MIX", 0, A)], lat={"s": 2.0}, rows=True)
-        sca(V("ST", 0, 3200), offu, V("MIX", 0, A))
+        primed(rnd)
+        rows([(2, V("MIX", 0, A), 2, V("LX", 0, A)), (3, V("MIX", 0, A), 3, V("LX", 0, A))])
+        sca(V("ST", 0, NT), offu, V("MIX", 0, A))
         if rnd == 0:
-            for t, a, b, c in (("JA", 0, A, 0), ("JA", 3840, P, 3840), ("JB", 0, A, 0), ("JB", 3840, P, 3840), ("RHO0", 0, 2048, 0), ("RHO0", 2048, P, 2048),
-                               ("RHO0", P, 4608, 0), ("RHO1", 0, 2048, 0), ("RHO1", 2048, P, 2048), ("RHO1", P, 4608, 0)):
+            for t, a, b, c in (("JA", 0, A, 0), ("JA", 3840, P, 3840), ("JB", 0, A, 0), ("JB", 3840, P, 3840),
+                               ("RHO", 0, 2048, 0), ("RHO", 2048, P, 2048), ("RHO", P, 5632, 0)):
                 dma(V(t, a, b), V("LX", P + c, P + c + b - a))
                 ops[-1]["rd"].append(V("MIX", 0, 8))
-        mm([(V("P0", 0, 320), V("DG1", 0, 128), V("ST", 2560, 2880)), (V("P0", 0, 320), V("DG2", 0, 128), V("ST", 1280, 1920, 2)),
-            (V("P0", 0, 320), V("DG3", 0, 128), V("ST", 1281, 1920, 2))], True)
-        cp(V("TT", 0, 320), V("P0", 0, 320), "a")
-        tt(isV, pf, cand, sub)
-        qm, qamA, qaA = w_(), w_(), w_()
-        aff(qm, qa, bias=-4096.0)
-        aff(qamA, qa, bias=-1.0 * A)
-        aff(qaA, qa, bias=1.0 * A)
-        tt(e1, ann, qm, mul)
-        tt(V("JAW", 0, 80), e1, B1, add_)
-        tt(V("JAW", 80, 160), e1, B2, add_)
-        dl, dlu = w_(), V("U", 240, 320)
-        tt(dl, ann, cmA, mul)
-        ts(dlu, dl, float(A), add_)
-        if rnd == 0:
-            ga(V("SA", A, 2 * A), V(X, A, 2576), dlu)
-            cp(V("SA", 2 * A, 3 * A), V("SA", A, 2 * A), "sga")
-            for c in range(2):
-                cp(V("SC", 640 * c, 640 * c + 640), V("SA", A + 640 * c, A + 640 * c + 640), "gsa")
         else:
-            slu = V("U", 320, 480)
-            ts(slu, V("JAW", 0, 160), float(Z), mn)
-            ga(V("DM", 0, A), V(X, A, 2576), dlu)
+            dma(V("RHO", 0, 2 * A), V("LX", P, P + 2 * A))
+        su, se, so = V("ST", UB, UB + 320), V("ST", FB, FB + 640, 2), V("ST", FB + 1, FB + 640, 2)
+        mm([(V("P0", 0, 320), m_("MV"), su), (V("P0", 0, 320), m_("M45"), so)], True)
+        relu(V("VT", 0, 320), V("P0", 0, 320), c_(12))
+        mm([(V("P1", 0, 320), m_("MU"), su), (V("P1", 0, 320), m_("M45"), se), (V("P1", 0, 320), m_("MB"), so)], True)
+        relu(V("TT", UB, UB + 320), V("P1", 0, 320), c_(11))
+        wrap(V("P5B", 0, 20), V("VT", 0, 320), "WV")
+        vl, vu, uu = V("TW", 0, 20), V("U", 160, 180), V("U", 180, 200)
+        tt(vl, V("P5B", 0, 20), V("KW", 64, 84), mn)
+        ts(vu, vl, float(P), add_)
+        sca(V("TT", 0, FB), vu, V("VT", 0, 320))
+        mm([(V("P2", 0, 320), m_("M89"), se), (V("P2", 0, 320), m_("MC"), so), (V("P2", 0, 320), m_("ME"), su)], True)
+        relu(V("TT", FB, FB + 640, 2), V("P2", 0, 320), c_(13))
+        mm([(V("P6B", 0, 320), m_("M89"), so), (V("P6B", 0, 320), m_("MC"), se), (V("P6B", 0, 320), m_("MO"), su)], True)
+        relu(V("TT", FB + 1, FB + 640, 2), V("P6B", 0, 320), c_(13))
+        tt(e1, ann, qm, mul)
+        tt(z, e1, col, add_)
+        dlu = V("U", 200, 280)
+        ts(dlu, z, 4096.0, add_, float(A), mn)
+        if rnd == 0:
+            for c in range(2):
+                o = V("SA", A + 640 * c, A + 640 * c + 640)
+                ga(o, V("DA", 0, KA), sub_(dlu, 40 * c, 40 * c + 40))
+                cp(V("SA", 2 * A + 640 * c, 2 * A + 640 * c + 640), o, "gsa")
+                cp(V("SC", 640 * c, 640 * c + 640), o, "gsa")
+        else:
+            slu = V("U", 280, 440)
+            for h in range(2):
+                ts(sub_(slu, 80 * h, 80 * h + 80), z, float(P + A + A * h), add_, float(P), mn)
+                ga(V("DM", 640 * h, 640 * h + 640), V("DA", 0, KA), sub_(dlu, 40 * h, 40 * h + 40))
             for c in range(4):
                 o = V("SA", A + 640 * c, A + 640 * c + 640)
-                gat(o, V("PH", 0, SS), sub_(slu, 40 * c, 40 * c + 40), V("DM", 640 * (c % 2), 640 * (c % 2) + 640), add_)
+                gat(o, V("PH", 0, P + 8), sub_(slu, 40 * c, 40 * c + 40), V("DM", 640 * (c % 2), 640 * (c % 2) + 640), add_)
                 cp(V("SC", 640 * c, 640 * c + 640), o, "sga" if c % 2 else "gsa")
-        cp(V("RI", 0, 81), V("RK", 1, 82))
-        ts(V("HF", 0, 81), V("RI", 0, 81), 1, ALU.arith_shift_right)
-        ts(V("OD", 0, 80), V("RI", 0, 80), 1, band)
-        odd, lim = V("OD", 0, 80), c_(9)
-        ts(lim, V("HF", 80, 81), 1920.0, add_, V("RK", 163, 164), mn)
-        nFm, nUF, t1, t2, dU, x1, s1 = (w_() for _ in range(7))
-        tlu = V("U", 560, 640)
-        ts(px[0], V("HF", 0, 80), 1920.0, add_)
-        tt(nFm, px[0], free, mul)
-        tt(nUF, V("PX", 83, 163), nFm, add_)
-        ts(act, nUF, lim, ALU.is_lt)
-        aff(t1, nUF, bias=-2880.0)
-        tt(t2, act, t1, mul)
-        ts(tlu, t2, 320.0, add_)
-        tt(dU, act, cand, mul)
-        tt(fus, act, free, mul)
-        tt(s1, ann, fus, add_)
         for h in range(2):
-            ga(V("TM", 640 * h, 640 * h + 640), V("TT", 0, 336), sub_(tlu, 40 * h, 40 * h + 40))
-        for h in range(2):
-            ga(V("TM2", 640 * h, 640 * h + 640), V("TM", 0, A), sub_(cu, 40 * h, 40 * h + 40))
-        wrap(V("P0", 0, 80), V("TM", 0, A), "W45")
-        wrap(V("P1", 0, 80), V("TM2", 0, A), "W67")
-        tt(x1, V("P0", 0, 80), cand, mul)
-        tt(px[0], V("P1", 0, 80), isV, mul)
-        ts(px[1], px[0], 0.0, ALU.is_gt)
-        tt(dbl, px[1], dU, add_)
-        j1, j2, e3, ju = w_(), w_(), w_(), V("U", 640, 800)
-        tt(px[2], dbl, qamA, mul)
-        tt(j1, px[2], V("JAW", 0, 80), add_)
-        cp(sub_(ju, 0, 80), j1)
-        tt(x1, x1, col2A, sub)
-        tt(e3, px[0], x1, add_)
-        tt(px[1], dbl, e3, mul)
-        tt(j2, px[1], V("JAW", 80, 160), add_)
-        cp(sub_(ju, 80, 160), j2)
+            ga(V("TM", 640 * h, 640 * h + 640), V("TT", 0, NT), sub_(offu, 40 * h, 40 * h + 40))
+        TM, ju = V("TM", 0, A), V("U", 440, 600)
+        for h, bk in ((0, "P0"), (1, "P1")):
+            wrap(V(bk, 0, 80), TM, "WD%d" % (h + 1), [(m_("I32"), z)])
+            ts(sub_(ju, 80 * h, 80 * h + 80), V(bk, 0, 80), float(P + A + A * h), add_)
         for h in range(4):
             ga(V("JA", A + 640 * h, A + 640 * h + 640), V("LX", 0, 2 * P), sub_(ju, 40 * h, 40 * h + 40))
-        tt(spec, dbl, s1, add_)
-        wrap(V("P2", 0, 80), V("TM", 0, A), "W01")
-        wrap(V("P3", 0, 80), V("TM", 0, A), "WD")
-        wrap(V("P4B", 0, 80), V("TM", 0, A), "WU")
-        g1, e5, g12, aq, l4, pa, b1, b2 = (w_() for _ in range(8))
-        tt(b1, V("P3", 0, 80), odd, mul)
-        tt(b2, V("P2", 0, 80), b1, add_)
-        aff(e5, e3, bias=3.0 * A)
-        tt(px[0], b2, cm2A, sub)
-        tt(b1, px[0], fus, mul)
-        tt(px[1], dbl, qaA, mul)
-        tt(g12, px[1], b1, add_)
-        tt(aq, ann, qa, mul)
-        tt(l4, col, g12, add_)
-        l4u = V("U", 800, 880)
-        cp(l4u, l4)
-        ga(V("TP", 0, A), V("LX", 0, P), l4u)
-        wrap(V("P1", 0, 80), V("TP", 0, A), "W23")
-        cp(V("L4U", 0, 80), V("P1", 0, 80))
-        tt(V("CL", 0, 160), colcol, V("LW", 80, 240), sub)
-        tt(px[2], spec, V("CL", 0, 80), mul)
-        tt(px[3], spec, V("CL", 80, 160), mul)
-        tt(V("L4", 80, 240), V("PX", 324, 484), V("LW", 80, 240), add_)
-        cp(V("L4U", 80, 240), V("L4", 80, 240))
-        cp(V("L4U", 240, 256), V("LW", 240, 256))
-        tt(px[0], V("P4B", 0, 80), c2m, sub)
-        tt(pa, px[0], fus, mul)
-        tt(px[1], dbl, e5, mul)
-        tt(g1, px[1], pa, add_)
-        ts(px[0], ann, float(A), mul)
-        ts(px[1], ann, 2.0 * A, mul)
-        tt(V("CC", 0, 80), px[0], g12, add_)
-        tt(V("CC", 80, 160), px[1], g1, add_)
+        l4u = V("U", 600, 680)
+        wrap(V("P2", 0, 80), TM, "WD3", [(m_("I1"), colA), (m_("IP"), ann)])
+        ts(l4u, V("P2", 0, 80), c_(1), add_)
+        if rnd:
+            aff(V("PL", 0, 80), V("P2", 0, 80), bias=c_(1))
+        ga(V("TP", 0, A), V("LX", 0, 2 * P), l4u)
+        wrap(V("P2", 0, 80), V("TP", 0, A), "WP")
+        cp(V("F4U", 0, 80), V("P2", 0, 80))
         if rnd == 0:
-            cp(V("L4", 0, 80), V("P1", 0, 80))
-            PL, pb = "L4", V("LW", 240, 256)
-        else:
-            tt(px[0], ann, V("CW", 560, 640), mul)
-            tt(V("P4", 0, 80), px[0], l4, add_)
-            tt(px[2], spec, V("CW", 640, 720), mul)
-            tt(px[3], spec, V("CW", 720, 800), mul)
-            tt(V("P4", 80, 240), V("PX", 324, 484), V("PW", 80, 240), add_)
-            cp(V("P5U", 160, 240), V("P4", 160, 240))
-            PL, pb = "P4", V("PW", 240, 256)
-        uu = V("U", 880, 900)
-        wrap(V("P5B", 0, 20), V("ST", 2560, 2880), "W01")
-        cp(uu, V("P5B", 0, 20))
-        ga(V("DU", 0, 320), V("DB", 0, A), uu)
-        ga(V("X2", 0, 320), V(X, 0, A), uu, scale=2.0)
-        ab(V(X, 2577, 3216, 2), V("DU", 0, 320))
-        tt(V("S1", 0, 320), V("DU", 0, 320), V("X2", 0, 320), add_)
-        ts(V("S2", 0, 320), V("S1", 0, 320), 16.0, ALU.is_ge, -16.0, mul)
-        tt(V(X, 2576, 3216, 2), V("S1", 0, 320), V("S2", 0, 320), add_)
-        xl, xm, xlu = w_(), w_(), V("U", 900, 980)
-        tt(px[0], valF, cm1296, sub)
-        tt(xl, px[0], fus, mul)
-        tt(xm, xl, col, add_)
+            cp(V("PL", 0, 80), V("P2", 0, 80), "av")
+        spec = V("P6B", 0, 80)
+        wrap(spec, TM, "WN", [(m_("I1"), ann)])
+        xm, xlu = w_(), V("U", 680, 760)
+        for h in range(2):
+            tt(V("CL", 80 * h, 80 * h + 80), col, V("LW", 80 + 80 * h, 160 + 80 * h), sub)
+            tt(V("TW", 80 * h, 80 * h + 80), spec, V("CL", 80 * h, 80 * h + 80), mul)
+        tt(px[1], spec, valF, mul)
+        if rnd:
+            aff(V("HB", 240, 320), spec, scale=float(PO), bias=float(A), engs="a")
+            aff(V("HB", 320, 400), spec, scale=float(P - 2 * A), bias=float(2 * A), engs="a")
+            mm([(V("P5B", 0, 80), m_("I1"), colA), (V("P5B", 0, 80), m_("I1"), V("HB", 240, 320))], True)
+            mm([(V("P5B", 80, 160), m_("I1"), colA), (V("P5B", 80, 160), m_("I1"), V("HB", 320, 400))], True)
+            aff(V("PL", 80, 160), V("P5B", 0, 80), bias=c_(1))
+            ts(V("P5U", 160, 240), V("P5B", 80, 160), c_(1), add_, float(2 * A), sub)
+        tt(xm, px[1], col, mx)
         cp(xlu, xm)
-        ga(V(XN, 0, A), V(X, 0, 3216), xlu)
-        banks = ("P3", "P4B", "P5B", "P2")
+        wrap(V("P3", 0, 80), TM, "WD3", [(m_("IA"), ann), (m_("I32"), V("LW", 80, 160)), (m_("I32"), V("TW", 0, 80))])
+        wrap(V("P3", 80, 160), TM, "WD4", [(m_("IA"), ann), (m_("IA"), ann), (m_("I32"), V("LW", 160, 240)), (m_("I32"), V("TW", 80, 160))])
+        cp(V("F4U", 80, 240), V("P3", 0, 160))
+        if rnd == 0:
+            cp(V("PL", 80, 160), V("P3", 0, 80), "av")
+        pb = V("LW", 240, 256) if rnd == 0 else V("PW", 240, 256)
+        wrap(V("P4B", 0, 20), V("VT", 0, 320), "W23")
+        cp(uu, V("P4B", 0, 20))
+        ga(V("X1", 0, 320), V(X, 0, A), uu)
+        ga(V(X, FB + 1, FB + 640, 2), V("DA", 0, A), uu)
+        gat(V("S1", 0, 320), V(X, 0, FB), vu, V("X1", 0, 320), add_)
+        ts(V("PX", 160, 480), V("S1", 0, 320), 16.0, ALU.is_ge, -16.0, mul)
+        tt(V(X, FB, FB + 640, 2), V("PX", 160, 480), V("S1", 0, 320), add_)
+        ga(V(XN, 0, A), V(X, 0, FB + 640), xlu)
+        banks = ("P0", "P1", "P4B", "P5B")
         for s in range(5):
-            jx, jy = ("JA", "JB") if s % 2 == 0 else ("JB", "JA")
-            sx, sy = ("SA", "SB") if s % 2 == 0 else ("SB", "SA")
+            jx, jy, jo = (("JA", "JB", A), ("JB", "JA", A), ("JA", "JB", A), ("JB", "JA", A), ("JA", "LX", 2 * P))[s]
+            sx, sy, so_ = (("SA", "SB", A), ("SB", "SA", A), ("SA", "SB", A), ("SB", "SA", A), ("SA", "SF", P))[s]
             for h in range(2):
                 bk = banks[(2 * s + h) % 4]
                 wrap(V(bk, 0, 80), V(jx, A + A * h, 2 * A + A * h), "W23")
                 cp(V("JU", 160 * s + 80 * h, 160 * s + 80 * h + 80), V(bk, 0, 80))
             for h in range(2):
-                ga(V(jy, A + A * h, 2 * A + A * h), V(jx, 0, P), V("JU", 160 * s + 80 * h, 160 * s + 80 * h + 80), "a")
-            for c in range(4):
-                o = V(sy, A + 640 * c, A + 640 * c + 640)
-                c0 = c % 2 if rnd == 0 and s == 0 else c
-                gat(o, V(sx, 0, P), V("JU", 160 * s + 40 * c, 160 * s + 40 * c + 40), V("SC", 640 * c0, 640 * c0 + 640), add_)
+                ga(V(jy, jo + A * h, jo + A + A * h), V(jx, 0, P), V("JU", 160 * s + 80 * h, 160 * s + 80 * h + 80), "a")
+            for a in range(0, 2 * A, SP):
+                b = a % A if rnd == 0 and s == 0 else a
+                gat(V(sy, so_ + a, so_ + a + SP), V(sx, 0, P), V("JU", 160 * s + a // 16, 160 * s + (a + SP) // 16), V("SC", b, b + SP), add_)
             for c in range(4 if s < 4 else 0):
                 cp(V("SC", 640 * c, 640 * c + 640), V(sy, A + 640 * c, A + 640 * c + 640), "sga" if c % 2 else "gsa")
-        JW = V("JB", 0, P)
-        ga(V("KT", KB, KB + NB), JW, V("L4U", 240, 256), "a")
+        JW, SW = V("LX", P, 2 * P + 2 * A), V("SF", 0, SS)
+        ga(V("KT", KB, KB + NB), JW, V("F4U", 240, 256), "a")
         for h in range(2):
-            ga(V("KT", 640 * h, 640 * h + 640), JW, V("L4U", 40 * h, 40 * h + 40))
+            ga(V("KT", 640 * h, 640 * h + 640), JW, V("F4U", 40 * h, 40 * h + 40))
         wrap(V("P0", 0, 16), V("KT", KB, KB + NB), "W23")
-        atu = V("U", 980, 996)
+        atu = V("U", 760, 776)
         ts(atu, V("P0", 0, 16), float(A), mn)
-        cp(V("K4", 240, 256), V("P0", 0, 16))
+        cp(V("L5U", 240, 256), V("P0", 0, 16))
+        cp(V("AW", 0, 16), V("P0", 0, 16), "av")
+        aff(V("AW", 16, 32), V("PW", 0, 16), bias=float((SS, QS)[rnd]))
         gat(V("EQ", 0, NB), V("KT", 0, KA), atu, V("LX", P + 3840, 2 * P), ALU.is_equal)
         wrap(V("P1", 0, 16), V("EQ", 0, NB), "W23")
         SF, RF, SX, RX, RP = ("%s%d" % (s, rnd) for s in ("SF", "RF", "SX", "RX", "RP"))
-        ts(V(SF, 0, 16), V("P1", 0, 16), 65.0, ALU.is_equal)
-        send(V(RF, 0, 16), V(SF, 0, 16), rnd)
+        for j in range(2):
+            ts(V(SF, 16 * j, 16 * j + 16), V("P1", 0, 16), 65.0, ALU.not_equal, (BIG, -BIG)[j], mul)
+        send(V(RF, 0, 32), V(SF, 0, 32), rnd)
+        tt(V("AW", 48, 80), V("AW", 0, 32), V(SF, 0, 32), add_)
         ga(V(SX, 0, NB), V(XN, 0, KA), atu)
         send(V(RX, 0, NB), V(SX, 0, NB), rnd)
         if rnd == 0:
             own = V("SP0", 0, NB)
-            ga(own, V("SB", 0, P), V("L4U", 240, 256))
+            ga(own, SW, V("F4U", 240, 256))
         else:
             own = V("Q", 3840, P)
-            gat(own, V("SB", 0, P), V("LU", 240, 256), V("PH", 3840, P), add_)
+            gat(own, SW, V("LU", 240, 256), V("PH", 3840, P), add_)
             ts(own, own, 15, band)
         send(V(RP, 0, NB), own, rnd)
         for h in range(2):
-            ga(V("KT", KA + A * h, KA + A * h + A), JW, V("L4U", 80 + 80 * h, 160 + 80 * h))
+            ga(V("KT", KA + A * h, KA + A * h + A), JW, V("F4U", 80 + 80 * h, 160 + 80 * h))
         wrap(V("P2", 0, 80), V("KT", 0, A), "W23")
         wrap(V("P3", 0, 80), V("KT", KA, KA + A), "W23")
         wrap(V("P4B", 0, 80), V("KT", KA + A, KB), "W23")
-        tt(V("K4", 0, 80), V("P2", 0, 80), aq, sub)
-        tt(V("K4", 80, 160), V("P3", 0, 80), V("CC", 0, 80), add_)
-        tt(V("K4", 160, 240), V("P4B", 0, 80), V("CC", 80, 160), add_)
-        cp(V("L5U", 160, 256), V("K4", 160, 256))
-        aff(V("VR", 0, NB), V("KT", KB, KB + NB), bias=c_(7 + rnd))
-        cp(V("VR", NB, 2 * NB), V("KT", KB, KB + NB), "gav")
-        tt(V("AW", 0, 16), V("K4", 240, 256), V("KW", 0, 16), sub)
-        aff(V("AW", 16, 32), V("AW", 0, 16), bias=1024.0)
-        aff(V("AW", 32, 48), V("AW", 0, 16), bias=2816.0)
-        tt(V("AW", 48, 64), V("KW", 48, 64), pb, sub)
-        for j in range(4):
-            tt(V("AW", 64 + 16 * j, 80 + 16 * j), V("AW", 16 * j, 16 * j + 16), V(SF, 0, 16), mul)
+        cp(V("K4", 0, 80), V("P2", 0, 80), "av")
+        cp(V("K4", 80, 160), V("P3", 0, 80), "av")
+        cp(V("L5U", 160, 240), V("P4B", 0, 80))
+        aff(V("VR", 0, NB), V("KT", KB, KB + NB), bias=c_(14))
         dlt, d1, d2, k2 = w_(), w_(), w_(), w_()
-        tt(dlt, V("K4", 80, 160), V("K4", 0, 80), sub)
-        tt(d1, V(PL, 80, 160), V(PL, 0, 80), sub)
-        aff(k2, V("K4", 0, 80), bias=float(SS - 3840))
-        tt(d2, k2, V(PL, 80, 160), sub)
+        tt(dlt, V("P3", 0, 80), V("K4", 0, 80), sub)
+        tt(d1, V("PL", 80, 160), V("PL", 0, 80), sub)
+        aff(k2, V("PL", 80, 160), scale=-1.0, bias=float((SS, QS)[rnd] - 3840))
+        tt(d2, V("P2", 0, 80), k2, add_)
         if rnd == 0:
-            ga(V("PH", 2 * A, 3 * A), V("SB", 0, P), V("L4U", 160, 240))
+            ga(V("PH", 2 * A, 3 * A), SW, V("F4U", 160, 240))
         else:
             for c in range(6):
                 o = V("Q", 640 * c, 640 * c + 640)
-                gat(o, V("SB", 0, P), V("LU", 40 * c, 40 * c + 40), V("PH", 640 * c, 640 * c + 640), add_)
+                gat(o, SW, V("LU", 40 * c, 40 * c + 40), V("PH", 640 * c, 640 * c + 640), add_)
                 ts(o, o, 15, band)
                 cp(V("JA", 640 * c, 640 * c + 640), o, "gv")
             cp(V("JA", 3840, P), own, "gv")
             for a in (2560, 3200):
-                ga(V("JB", a, a + 640), V("JA", 0, SS), V("P5U", a // 16, a // 16 + 40))
+                ga(V("JB", a, a + 640), V("JA", 2 * A, QS), V("P5U", a // 16, a // 16 + 40))
                 dma(("yp", a, a + 640, 1), V("JB", a, a + 640))
-        for j in range(2):
-            tt(V("BW", 16 * j, 16 * j + 16), V("AW", 64 + 16 * j, 80 + 16 * j), V(RF, 0, 16), mul)
-        tt(V("BW", 64, 96), V("BW", 0, 32), V("KW", 0, 32), add_)
-        cp(V("OU", 0, 32), V("BW", 64, 96))
-        sca(V(RHO, 0, 4608), V("OU", 0, 32), V("VR", 0, 512))
-        wrap(V("P0", 0, 80), V(RHO, 0, A), "WF%d" % rnd)
-        for j in range(2, 4):
-            tt(V("BW", 16 * j, 16 * j + 16), V("AW", 64 + 16 * j, 80 + 16 * j), V(RF, 0, 16), mul)
-        tt(V("BW", 96, 112), V("BW", 32, 48), V("KW", 32, 48), add_)
-        cp(V("OU", 32, 48), V("BW", 96, 112))
+        tt(V("PX", 480, 512), V("AW", 48, 80), V(RF, 0, 32), add_)
+        tt(V("BW", 64, 80), V("PX", 480, 496), V("KW", 0, 16), mn)
+        cp(V("OU", 0, 16), V("BW", 64, 80))
+        sca(V(RHO, 0, P + NB), V("OU", 0, 16), V("VR", 0, NB))
+        sca(V(RHO, A, 5632), V("OU", 0, 16), V("KT", KB, KB + NB))
+        wrap(V("P0", 0, 80), V(RHO, 0, A), "WF")
+        tt(V("BW", 96, 112), V("PX", 480, 496), V("KW", 32, 48), mn)
+        tt(V("BW", 112, 128), V("PX", 496, 512), pb, mx)
+        cp(V("OU", 32, 64), V("BW", 96, 128))
         sca(V(XN, 0, 1536), V("OU", 32, 48), V(RX, 0, NB))
-        tt(V("P5", 240, 256), V("BW", 48, 64), pb, add_)
-        cp(V("P5U", 240, 256), V("P5", 240, 256))
         sw = V("P0", 0, 80)
-        tt(px[0], sw, dlt, mul)
-        tt(V("L5", 0, 80), px[0], V("K4", 0, 80), add_)
-        cp(V("L5U", 0, 80), V("L5", 0, 80))
-        tt(V("L5", 80, 160), V("K4", 80, 160), px[0], sub)
-        cp(V("L5U", 80, 160), V("L5", 80, 160))
-        tt(px[1], sw, d1, mul)
-        tt(px[2], sw, d2, mul)
-        tt(V("P5", 0, 160), V("PX", 244, 404), V(PL, 0, 160), add_)
-        cp(V("P5U", 0, 160), V("P5", 0, 160))
+        t0, t1, t2 = w_(), V("CL", 0, 80), V("CL", 80, 160)
+        tt(t0, sw, dlt, mul)
+        tt(px[0], t0, V("K4", 0, 80), add_)
+        cp(V("L5U", 0, 80), px[0])
+        tt(px[1], V("K4", 80, 160), t0, sub)
+        cp(V("L5U", 80, 160), px[1])
+        tt(t1, sw, d1, mul)
+        tt(t2, sw, d2, mul)
+        tt(V("PX", 160, 320), V("CL", 0, 160), V("PL", 0, 160), add_)
+        cp(V("P5U", 0, 160), V("PX", 160, 320))
         RW = V(RHO, 0, P)
         if rnd == 0:
             for a in (0, 640):
-                cp(V("X5", a, a + 640), V("XB", a, a + 640), "gsva")
-            tt(V("SB", SS, SS + NB), own, V(RP, 0, NB), add_)
+                cp(V("XA", a, a + 640), V("XB", a, a + 640), "gsva")
+            tt(V("SF", SS, SS + NB), own, V(RP, 0, NB), add_)
             for h in range(2):
                 ga(V("LX", 640 * h, 640 * h + 640), RW, V("L5U", 40 * h, 40 * h + 40))
             wrap(V("P1", 0, 80), V("LX", 0, A), "W23")
             ts(cu, V("P1", 0, 80), 1279.0, mn)
-            cp(V("LW", 0, 80), V("P1", 0, 80))
-            ga(V("LX", 2 * A, P), RW, V("L5U", 160, 256))
-            ga(V("LX", A, 2 * A), RW, V("L5U", 80, 160))
-            wrap(V("P2", 0, 96), V("LX", 2 * A, P), "W23")
-            wrap(V("P3", 0, 80), V("LX", A, 2 * A), "W23")
-            cp(V("LW", 160, 256), V("P2", 0, 96), "a")
-            cp(V("LW", 80, 160), V("P3", 0, 80), "a")
-            cp(V("LU", 0, 256), V("LW", 0, 256))
-            SW = V("SB", 0, 4360)
-            ga(V("PH", A, 2 * A), SW, V("P5U", 80, 160))
-            ga(V("PH", 0, A), SW, V("P5U", 0, 80))
-            ga(V("PH", 3840, P), SW, V("P5U", 240, 256))
+            cp(V("LW", 0, 80), V("P1", 0, 80), "va")
+            for a, b in ((2560, 3328), (3328, P), (A, 1920), (1920, 2560)):
+                ga(V("LX", a, b), RW, V("L5U", a // 16, b // 16))
+            SW = V("SF", 0, SS + NB)
+            for a in (A, 1920, 0, 640):
+                ga(V("PH", a, a + 640), SW, V("P5U", a // 16, a // 16 + 40))
+            ga(V("PH", 3840, P), SW, V("OU", 48, 64))
         else:
             dma(("yx", 0, A, 1), V(XN, 0, A))
-            qs = V("Q", SS, SS + NB)
+            qs = V("Q", P, P + NB)
             tt(qs, own, V(RP, 0, NB), add_)
             ts(qs, qs, 15, band)
-            cp(V("JA", SS, SS + NB), qs, "vg")
+            cp(V("JA", QS, QS + NB), qs, "vg")
             for a, b in ((3840, P), (0, 640), (640, A), (A, 1920), (1920, 2560)):
-                ga(V("JB", a, b), V("JA", 0, 4360), V("P5U", a // 16, b // 16))
+                ga(V("JB", a, b), V("JA", 0, QS + NB), V("P5U", a // 16, b // 16) if a < 3840 else V("OU", 48, 64))
                 dma(("yp", a, b, 1), V("JB", a, b))
             for a, b in ((2560, 3328), (3328, P), (0, 768), (768, A), (A, 2048), (2048, 2560)):
                 ga(V("LX", a, b), RW, V("L5U", a // 16, b // 16))
             for n, i in enumerate(list(range(10, 16)) + list(range(10))):
                 add("blk", "p", {"p": 0.02 + 256 * PCY}, [V("LX", 256 * i, 256 * i + 256), V("W23", 0, 144)], [V("P1", 0, 256)],
                     i=i, start=n == 0, stop=n == 15)
-            cp(V("YL", 0, 256), V("P1", 0, 256), "a")
-            dma(("yl", 0, P, 1), V("YL", 0, 256))
+            cp(V("RP0", 0, 256), V("P1", 0, 256), "a")
+            dma(("yl", 0, P, 1), V("RP0", 0, 256))
     return ops
 
 
@@ -522,60 +539,76 @@ def graph(ops):
         acc = [(r, False) for r in o["rd"]] + [(w, True) for w in o["wr"]]
         for v, w in acc:
             for m, a, b, pw in seen.get(v[0], []):
-                if ((w or pw) and a < v[2] and v[1] < b) or (v[0] in PSUM and ops[m]["engs"] != o["engs"]):
+                if ((w or pw) and a < v[2] and v[1] < b) or (v[0] in PSUM and (ops[m]["engs"] != o["engs"] or len(o["engs"]) > 1)):
                     dep.add(m)
         for v, w in acc:
             lst = seen.setdefault(v[0], [])
-            if w and v[3] == 1 and (v[0] not in PSUM or v[0] in ("PV", "PX")):
+            if w and v[3] == 1 and (v[0] not in PSUM or v[0] == "PX"):
                 lst[:] = [x for x in lst if not (v[1] <= x[1] and x[2] <= v[2])]
             lst.append((n, v[1], v[2], w))
         dep.discard(n)
         o["dep"] = sorted(dep)
 
 
-def schedule(cost, lat, pred, succ, pr, eng, back):
-    n = len(cost)
-    left = [len(x) for x in pred]
-    rdy = [lat[i].get(eng[i], 0.0) if back else 0.0 for i in range(n)]
+def replay(seq, pred, c, la, eng):
+    n = len(seq)
+    fin = [0.0] * n
     bind = [-1] * n
-    ready = {e: [] for e in "vapgs"}
-    for i in range(n):
-        if left[i] == 0:
-            ready[eng[i]].append(i)
-    free = {e: 0.0 for e in "vapgs"}
-    prev = {e: -1 for e in "vapgs"}
-    out = []
-    end, last = 0.0, -1
+    free = [0.0] * 5
+    prev = [-1] * 5
+    end, last, tot = 0.0, -1, 0.0
+    for i in seq:
+        e = eng[i]
+        st = free[e]
+        b = prev[e]
+        for d in pred[i]:
+            if fin[d] > st:
+                st = fin[d]
+                b = d
+        bind[i] = b
+        st += c[i]
+        free[e] = st
+        prev[e] = i
+        st += la[i]
+        fin[i] = st
+        tot += st
+        if st > end:
+            end, last = st, i
+    return end, tot, fin, bind, last
+
+
+def greedy(c, la, pred, succ, pr, eng, back):
+    n = len(c)
+    left = [len(x) for x in pred]
+    rdy = list(la) if back else [0.0] * n
+    ready = [[i for i in range(n) if left[i] == 0 and eng[i] == e] for e in range(5)]
+    free = [0.0] * 5
+    nxt = {e: min([rdy[i] for i in ready[e]]) for e in range(5) if ready[e]}
+    seq, fin = [], [0.0] * n
     for _ in range(n):
-        t0, e = min((max(free[x], min([rdy[i] for i in ready[x]])), x) for x in "vapgs" if ready[x])
+        e = min(nxt, key=nxt.get)
+        t0 = nxt[e]
         i = max([(pr[j], j) for j in ready[e] if rdy[j] <= t0 + SLACK])[1]
         ready[e].remove(i)
-        if free[e] > rdy[i]:
-            bind[i] = prev[e]
-        st = max(t0, rdy[i])
-        free[e] = st + cost[i][e]
-        prev[e] = i
-        fin = free[e] + (0.0 if back else lat[i].get(e, 0.0))
-        if fin > end:
-            end, last = fin, i
-        out.append((i, e, st, fin))
-        fin += LAT
+        free[e] = max(t0, rdy[i]) + c[i]
+        if ready[e]:
+            nxt[e] = max(free[e], min([rdy[j] for j in ready[e]]))
+        else:
+            del nxt[e]
+        fin[i] = free[e] if back else free[e] + la[i]
+        seq.append(i)
         for s in succ[i]:
-            f = fin + lat[s].get(eng[s], 0.0) if back else fin
-            if f > rdy[s]:
-                rdy[s] = f
-                bind[s] = i
+            rdy[s] = max(rdy[s], fin[i] + la[s] if back else fin[i])
             left[s] -= 1
             if left[s] == 0:
-                ready[eng[s]].append(s)
-    chain = []
-    while last >= 0:
-        chain.append(last)
-        last = bind[last]
-    return end, out, chain
+                x = eng[s]
+                ready[x].append(s)
+                nxt[x] = min(nxt.get(x, 1e9), max(rdy[s], free[x]))
+    return seq, fin
 
 
 PLAN = {}
+ENG = "vapgs"
 
 
 def plan():
@@ -583,41 +616,73 @@ def plan():
         ops = build()
         graph(ops)
         n = len(ops)
-        pred = [o["dep"] for o in ops]
-        succ = [[] for _ in range(n)]
+        anc, pred, succ = [0] * n, [], [[] for _ in range(n)]
         for i, o in enumerate(ops):
+            cover = 0
             for d in o["dep"]:
+                cover |= anc[d]
+            pred.append([d for d in o["dep"] if not cover >> d & 1])
+            for d in pred[i]:
                 succ[d].append(i)
-        cost, lat = [o["cost"] for o in ops], [o["lat"] for o in ops]
-        eng = [o["engs"][0] for o in ops]
+                cover |= 1 << d
+            anc[i] = cover
+        alt = [[ENG.index(x) for x in o["engs"]] for o in ops]
+        eng = [x[0] for x in alt]
+        c = [ops[i]["cost"][ENG[eng[i]]] for i in range(n)]
+        la = [ops[i]["lat"].get(ENG[eng[i]], 0.0) + LAT for i in range(n)]
         pr = [0.0] * n
         for i in range(n - 1, -1, -1):
-            pr[i] = cost[i][eng[i]] + lat[i].get(eng[i], 0.0) + LAT + max([pr[s] for s in succ[i]] + [0.0])
-        flex = [i for i in range(n) if len(ops[i]["engs"]) > 1]
-        cur = best = schedule(cost, lat, pred, succ, pr, eng, False)
-        rs = np.random.RandomState(1)
+            pr[i] = c[i] + la[i] + max([pr[s] for s in succ[i]] + [0.0])
+        rs = np.random.RandomState(SEED)
+        seq, fin = greedy(c, la, pred, succ, pr, eng, False)
+        flex = [i for i in range(n) if len(alt[i]) > 1]
         for t in range(TRIES):
-            e2 = list(eng)
-            fl = [i for i in cur[2] if len(ops[i]["engs"]) > 1]
-            u = rs.uniform()
-            if u < 0.7:
-                f = fl[int(rs.randint(len(fl)))] if u < 0.4 and fl else flex[int(rs.randint(len(flex)))]
-                other = ops[f]["engs"].replace(e2[f], "")
-                e2[f] = other[int(rs.randint(len(other)))]
-            p2 = [0.0] * n
-            for i, _e, _s, fin in cur[1]:
-                p2[i] = fin
-            for i in rs.randint(n, size=int(rs.randint(6))):
-                p2[int(i)] += float(rs.normal()) * 1.5
-            for i, _e, _s, fin in schedule(cost, lat, succ, pred, p2, e2, True)[1]:
-                p2[i] = fin
-            s = schedule(cost, lat, pred, succ, p2, e2, False)
-            if s[0] <= cur[0] + 0.5 * (1.0 - t / TRIES) * rs.uniform():
-                cur, eng = s, e2
-                if s[0] < best[0]:
-                    best = s
-        PLAN["ops"], PLAN["end"], PLAN["order"], PLAN["ch"] = ops, best[0], best[1], best[2]
-    return PLAN["ops"], PLAN["order"]
+            i = flex[int(rs.randint(len(flex)))]
+            oe, oc, ol = eng[i], c[i], la[i]
+            ne = alt[i][int(rs.randint(len(alt[i])))]
+            eng[i], c[i], la[i] = ne, ops[i]["cost"][ENG[ne]], ops[i]["lat"].get(ENG[ne], 0.0) + LAT
+            s2, f2 = greedy(c, la, pred, succ, greedy(c, la, succ, pred, fin, eng, True)[1], eng, False)
+            if max(f2) <= max(fin) + 0.5 * (1.0 - t / TRIES) * rs.uniform():
+                seq, fin = s2, f2
+            else:
+                eng[i], c[i], la[i] = oe, oc, ol
+        end, tot, fin, bind, last = replay(seq, pred, c, la, eng)
+        cur = end + 0.05 * tot / n
+        best = (end, list(seq), list(eng))
+        pos = [0] * n
+        chain = None
+        rnd = rs.uniform(size=(STEPS, 7)).tolist()
+        for t in range(STEPS):
+            if chain is None:
+                chain = []
+                x = last
+                while x >= 0:
+                    chain.append(x)
+                    x = bind[x]
+                for p, i in enumerate(seq):
+                    pos[i] = p
+            u0, u1, u2, u3, u4, u5, u6 = rnd[t]
+            i = chain[int(u1 * len(chain))] if u0 < 0.6 else int(u1 * n)
+            p, oe = pos[i], eng[i]
+            ne = alt[i][int(u3 * len(alt[i]))] if u2 < 0.35 else oe
+            w = 1 + int(40 * u4 * u4 * u4) if u2 > 0.1 else 0
+            q = max(p - w, max([pos[d] for d in pred[i]] + [-1]) + 1) if u5 < 0.5 else min(p + w, min([pos[s] for s in succ[i]] + [n]) - 1)
+            if q == p and ne == oe:
+                continue
+            s2 = seq[:p] + seq[p + 1:]
+            s2.insert(q, i)
+            oc, ol = c[i], la[i]
+            eng[i], c[i], la[i] = ne, ops[i]["cost"][ENG[ne]], ops[i]["lat"].get(ENG[ne], 0.0) + LAT
+            e2, t2, f2, b2, l2 = replay(s2, pred, c, la, eng)
+            v = e2 + 0.05 * t2 / n
+            if v <= cur or u6 < math.exp((cur - v) / (HEAT * (1.0 - t / STEPS) ** 2 + 1e-4)):
+                seq, cur, bind, last, chain = s2, v, b2, l2, None
+                if e2 < best[0]:
+                    best = (e2, list(seq), list(eng))
+            else:
+                eng[i], c[i], la[i] = oe, oc, ol
+        PLAN["ops"], PLAN["end"], PLAN["seq"], PLAN["eng"], PLAN["pred"] = ops, best[0], best[1], best[2], pred
+    return PLAN["ops"], [(i, ENG[PLAN["eng"][i]]) for i in PLAN["seq"]]
 
 
 def rank_program(g, core, T, topo):
@@ -640,7 +705,7 @@ def rank_program(g, core, T, topo):
     known = {e: {} for e in Q}
     done = {}
     nd = 0
-    for i, e, _st, _fin in order:
+    for i, e in order:
         o = ops[i]
         kind = o["kind"]
         k = {n: ap(v) for n, v in o["k"].items()}
@@ -648,7 +713,7 @@ def rank_program(g, core, T, topo):
         kn = known[e]
         need = {}
         for d in o["dep"]:
-            if kind == "blk" and ops[d]["kind"] == "blk":
+            if (kind == "blk" and ops[d]["kind"] == "blk") or d == k.get("prev"):
                 continue
             sem, val, snap = done[d]
             if need.get(sem, (0, None))[0] < val:
@@ -665,11 +730,11 @@ def rank_program(g, core, T, topo):
             sem = "d%d" % nd
             nd += 1
             if "rows" in k:
-                for r0 in (2, 3):
-                    q.dma_start(T.MIX[r0:128:16, 0:A], T.LX[r0:128:16, 0:A]).then_inc(T.sem[sem], 16)
+                for ro, vo, ri, vi in k["rows"]:
+                    q.dma_start(T[vo[0]][ro:128:16, vo[1]:vo[2]], T[vi[0]][ri:128:16, vi[1]:vi[2]]).then_inc(T.sem[sem], 16)
             else:
                 q.dma_start(k["o"], k["i"]).then_inc(T.sem[sem], 16)
-            total[sem] = 32 if "rows" in k else 16
+            total[sem] = 16 * len(k["rows"]) if "rows" in k else 16
             done[i] = (sem, total[sem], dict(kn))
             continue
         if kind == "send":
@@ -703,21 +768,24 @@ def rank_program(g, core, T, topo):
                 r = q.tensor_scalar(k["o"], k["i"], k["scale"], k["bias"], ALU.mult, ALU.add)
         elif kind == "abs":
             r = q.activation(k["o"], k["i"], ACT.Abs, bias=k["bias"])
-        elif kind == "tri":
-            r = q.affine_select(k["o"], k["i"], [[-1, 128]], ALU.is_ge, 0.0, 0, 1)
-        elif kind == "ga":
+        elif kind == "relu":
             if e == "a":
-                r = q.activation(k["o"], ind, ACT.Copy) if k["scale"] is None else q.activation(k["o"], ind, ACT.Identity, scale=k["scale"])
+                r = q.activation(k["o"], k["i"], ACT.Relu, bias=k["bias"])
             else:
-                r = q.tensor_copy(k["o"], ind) if k["scale"] is None else q.tensor_scalar(k["o"], ind, k["scale"], None, ALU.mult)
+                r = q.tensor_scalar(k["o"], k["i"], k["bias"], 0.0, ALU.add, ALU.max)
+        elif kind == "tri":
+            r = q.affine_select(k["o"], k["i"], [[-1, 128]], ALU.is_gt, 0.0, 0, 1)
+        elif kind == "ga":
+            r = q.activation(k["o"], ind, ACT.Copy) if e == "a" else q.tensor_copy(k["o"], ind)
         elif kind == "gat":
             r = q.tensor_tensor(k["o"], ind, k["b"], k["op"])
         elif kind == "sca":
             r = q.tensor_copy(ind, k["i"])
         elif kind == "wrap":
             t = o["k"]["t"]
-            for j in range(16):
-                r = q.matmul(k["o"], T[k["m"]][:, 15 - j:143 - j], T[t[0]][:, t[1] + j:t[2]:16], j == 0, j == 15)
+            ms = [(ap(l), ap(rr)) for l, rr in k["extra"]] + [(T[k["m"]][:, 15 - j:143 - j], T[t[0]][:, t[1] + j:t[2]:16]) for j in range(16)]
+            for j, (l, rr) in enumerate(ms):
+                r = q.matmul(k["o"], l, rr, k["start"] and j == 0, k["stop"] and j == len(ms) - 1)
         elif kind == "blk":
             j = k["i"]
             r = q.matmul(T.P1[:, 0:256], T.W23[:, 15 - j:143 - j], T.LX[:, 256 * j:256 * j + 256], k["start"], k["stop"])
@@ -725,7 +793,11 @@ def rank_program(g, core, T, topo):
             for j, (oo, l, rr) in enumerate(k["items"]):
                 r = q.matmul(ap(oo), ap(l), ap(rr), j == 0 or not k["acc"], j == len(k["items"]) - 1 or not k["acc"])
         elif kind == "scan":
-            r = q.tensor_tensor_scan(k["o"], k["a"], k["b"], 0.0, ALU.mult, ALU.add)
+            r = q.tensor_tensor_scan(k["o"], k["a"], k["b"], k["init"], ALU.mult, ALU.add)
+        elif kind == "ms" and e == "v":
+            r = q.memset(k["o"], 0.0)
+        elif kind == "ms":
+            r = q.iota(k["o"], [[0, width(o["k"]["o"])]], 0, 0, allow_small_or_imprecise_dtypes=True)
         elif SCRATCH[o["k"]["o"][0]][2] == I32:
             r = q.iota(k["o"], k["pat"], k["base"], k["cm"])
         else:

import math
import numpy as np
from concourse.mybir import AluOpType as ALU, ActivationFunctionType as ACT

A, NB, P = 1280, 256, 4096
XM = (1, 2)
PO = 2816
FB, UB, NT = 1600, 2881, 3536
KA, KB = 1296, 3856
SS, QS = 6656, 5376
BIG = 8192.0
SP = 640

BF, F32, I32, U16 = "bfloat16", "float32", "int32", "uint16"
WN = ("W23", "WP", "WD1", "WD2", "WD3", "WD4", "WN", "WV", "WF")
SIG = ({1: 1}, {1: 1, 2: 44}, {0: -1, 1: 1, 3: -20}, {0: -1, 2: 1, 3: -40}, {0: -1, 1: 1, 3: 20, 4: -1, 5: 1, 7: 40},
       {0: -1, 2: 1, 3: 20, 4: -1, 6: 1, 7: 40}, {3: 1, 7: 1}, {0: 1, 3: -64}, {4: 1})
MN = ("MU", "M45", "MB", "MV", "M89", "MC", "ME", "MO")
SHF = ((0, 0), (4, -999), (-999, -999), (2, -2), (8, -999), (12, -999), (10, -999), (-999, 8))
SCRATCH = {}
for _d, _l in (
        (I32, "LK:256 THI:2 Q:4352 RP1:256 PI:6"),
        (BF, "THB:2 LX:10752 JA:5632 JB:4096 KT:4112 RHO:5632 ST:3536 TT:3536 VT:320 XA:2240 XB:2240 DA:1296 "
             "DM:1280 MIX:1280 TP:1280 TM:1280 X1:320 S1:320 EQ:256 VR:256 SX0:256 SX1:256 RX0:256 RX1:256 WS:144 WM:144 "
             "ONES:128 TRI:128 TR0:128 I1:128 IA:128 IP:128 NI:128 TQ:128 FL:164 HB:400 " + " ".join(w + ":144" for w in WN) + " " + " ".join(m + ":128" for m in MN)),
        (F32, "TH:10 SA:4096 SB:4096 SF:6912 PH:4104 SP0:256 RP0:256 SF0:32 SF1:32 RF0:32 RF1:32 R:144 C:24 E:16 HI2:64 "
              "PW:256 KW:96 I32:128 MB2:128 D0:164 SN:164 RK:164 LW:256 PL:160 K4:160 W:1280 CL:160 TW:160 AW:96 BW:128 "
              "CW:9 CT:8 SC:2560"),
        (U16, "LU:256 F4U:256 L5U:256 P5U:256 JU:800 U:800 OU:64")):
    for _x in _l.split():
        SCRATCH[_x.split(":")[0]] = ("sbuf", [128, int(_x.split(":")[1])], _d)
PSUM = ("P0", "P1", "P2", "P3", "P4B", "P5B", "P6B", "PX")
for _n in PSUM:
    SCRATCH[_n] = ("psum", [128, 512], F32)
SEMAPHORES = ["cv", "ca", "cp", "cg", "sent"] + ["d%d" % i for i in range(110)] + ["arr%d" % i for i in range(6)]

CY, PCY = 0.83e-3, 0.83e-3
GA, SCA, FIX, BW, LAT, DL, RL = 1.56, 3.8, 0.05, 190e3, 0.06, 2.0, 2.5
STEPS, HEAT, TRIES, SLACK, SEED = 350000, 0.3, 1000, 0.12, 1


def V(n, a, b, s=1):
    return (n, a, b, s)


def width(v):
    return (v[2] - v[1] + v[3] - 1) // v[3]


def narrow(v):
    return SCRATCH[v[0]][2] in (BF, U16)


def build():
    ops = []

    def add(kind, engs, cost, rd, wr, lat=None, **k):
        ops.append({"kind": kind, "engs": engs, "cost": cost, "rd": [r for r in rd if isinstance(r, tuple) and r[0] in SCRATCH],
                    "wr": [w for w in wr if w[0] in SCRATCH], "k": k, "lat": lat or {}})

    def plain(o, i):
        n = width(o)
        by = n * (2 if narrow(o) else 4) * 128
        return {"v": FIX + max(64, n * (0.5 if narrow(o) and narrow(i) else 1)) * CY, "a": 0.1 + max(64, n) * CY,
                "g": 0.17 + 2 * n * CY, "s": 0.06 + by / BW}

    def ts(o, i, s1, op0, s2=None, op1=None):
        add("ts", "v", plain(o, i), [i, s1, s2], [o], o=o, i=i, s1=s1, s2=s2, op0=op0, op1=op1)

    def tt(o, a, b, op):
        c = width(o) * (1 if (a[0] in PSUM or b[0] in PSUM) else 2)
        add("tt", "v", {"v": FIX + max(64, c) * CY}, [a, b], [o], o=o, a=a, b=b, op=op)

    def cp(o, i, engs="v"):
        add("cp", engs, plain(o, i), [i], [o], lat={"s": DL}, o=o, i=i)

    def aff(o, i, bias=0.0, scale=1.0, engs="av"):
        add("aff", engs, plain(o, i), [i, bias, scale], [o], o=o, i=i, bias=bias, scale=scale)

    def ab(o, i, bias=0.0):
        add("abs", "a", plain(o, i), [i, bias], [o], o=o, i=i, bias=bias)

    def relu(o, i, bias):
        add("relu", "av", plain(o, i), [i, bias], [o], o=o, i=i, bias=bias, scale=1.0)

    def ga(o, w, l, engs="av"):
        n = width(o)
        add("ga", engs, {"v": 0.05 + n * GA * CY, "a": 0.065 + n * GA * CY}, [w, l], [o], o=o, w=w, l=l, scale=None)

    def gat(o, w, l, b, op):
        add("gat", "v", {"v": 0.05 + width(o) * GA * CY}, [w, l, b], [o], o=o, w=w, l=l, b=b, op=op)

    def sca(w, l, i):
        add("sca", "v", {"v": 0.05 + width(i) * SCA * CY}, [l, i], [w], w=w, l=l, i=i)

    def wrap(o, t, m, extra=(), start=True, stop=True, prev=None):
        c = 16 * max(64, width(o)) + sum(max(64, width(o)) * (1 if narrow(r) else 4) for _l, r in extra)
        add("wrap", "p", {"p": 0.05 + c * PCY}, [t, V(m, 0, 144)] + [x for y in extra for x in y], [o],
            o=o, t=t, m=m, extra=list(extra), start=start, stop=stop, prev=prev)
        return len(ops) - 1

    def mm(items, acc):
        add("mm", "p", {"p": 0.05 + sum(max(64, width(x[0])) for x in items) * PCY}, [x[1] for x in items] + [x[2] for x in items],
            [x[0] for x in items], items=items, acc=acc)

    def scan(o, a, b, init):
        add("scan", "v", plain(o, o), [a, b], [o], o=o, a=a, b=b, init=init)

    def io(o, pat, base, cm):
        add("iota", "g", {"g": 0.13 + 2 * width(o) * CY}, [], [o], o=o, pat=pat, base=base, cm=cm)

    def zero(o, engs="g"):
        c = plain(o, o)
        add("ms", engs, {"g": 0.13 + 2 * width(o) * CY, "v": c["v"]}, [], [o], o=o, c=0.0)

    def dma(o, i, eng="s"):
        v = o if o[0] in SCRATCH else i
        add("cp", eng, {"s": plain(v, v)["s"], "a": 0.06}, [i], [o], lat={"s": DL, "a": DL}, o=o, i=i, dma=True)

    def rows(lst):
        add("cp", "s", {"s": 0.12 * len(lst)}, [x[3] for x in lst], [x[1] for x in lst], lat={"s": DL}, rows=lst)

    nr = [0]

    def send(o, i, rnd):
        by = width(i) * (2 if narrow(i) else 4) * 128
        add("send", "g", {"g": 0.3}, [i], [o], lat={"g": RL + by / 80e3}, o=o, i=i, rnd=rnd, sem="arr%d" % nr[0])
        nr[0] += 1

    def c_(j):
        return V("C", j, j + 1)

    def e_(j):
        return V("E", j, j + 1)

    def sub_(v, a, b):
        return V(v[0], v[1] + a, v[1] + b)

    def m_(n):
        return V(n, 0, 128)

    add_, sub, mul, mx, mn, band = ALU.add, ALU.subtract, ALU.mult, ALU.max, ALU.min, ALU.bitwise_and
    IOT = V("LX", P, 2 * P)
    X0 = V("Q", 0, A)

    dma(V("LK", 0, 256), ("lk", 0, 256, 1))
    dma(X0, ("x0", 0, A, 1))
    dma(V("THI", 0, 2), ("th", 0, 2, 1), "a")
    io(V("PI", 0, 1), [[0, 1]], 0, 1)
    io(V("R", 0, 144), [[1, 144]], 0, 0)
    io(V("PW", 0, 256), [[16, 256]], 0, 1)
    for j, b in ((1, 15), (2, 112), (3, 14), (4, 1)):
        ts(V("PI", j, j + 1), V("PI", 0, 1), b, band)
    cp(V("C", 0, 5), V("PI", 0, 5))
    ts(V("E", 0, 16), V("R", 0, 16), c_(1), ALU.is_equal)
    ts(V("HI2", 0, 64), V("R", 0, 64), e_(2), mul)
    ts(V("LX", P, P + 64), V("R", 0, 64), e_(3), mul)
    n = 64
    while n < A:
        m = min(n, A - n)
        aff(V("LX", P + n, P + n + m), V("LX", P, P + m), bias=V("HI2", n // 64, n // 64 + 1), engs="v")
        n *= 2
    aff(c_(5), e_(2), scale=20.0, bias=e_(4))
    aff(c_(6), e_(2), scale=40.0, bias=e_(4))
    aff(V("LX", P + A, P + 2 * A), V("LX", P, P + A), bias=c_(5), engs="va")
    aff(V("LX", P + 2 * A, P + 3 * A), V("LX", P, P + A), bias=c_(6), engs="va")
    aff(V("LX", P + 3 * A, 2 * P), V("LX", P, P + NB), bias=V("HI2", 60, 61), engs="va")
    zero(V("MIX", 0, A), "gv")
    rows([(0, V("MIX", 0, A), 2, V("LX", P, P + A)), (1, V("MIX", 0, A), 3, V("LX", P, P + A)), (6, V("MIX", 0, A), 4, V("LX", P + A, P + 2 * A))])
    zero(V("W", 0, 136))
    for j, sg in enumerate(SIG):
        ks = sorted(sg)
        while ks:
            if len(ks) > 1 and ks[1] == ks[0] + 1:
                io(V("W", 8 * j + ks[0], 8 * j + ks[0] + 2), [[sg[ks[1]] - sg[ks[0]], 2]], sg[ks[0]], 0)
                ks = ks[2:]
            else:
                io(V("W", 8 * j + ks[0], 8 * j + ks[0] + 1), [[0, 1]], sg[ks[0]], 0)
                ks = ks[1:]
    io(V("W", 75, 136, 8), [[0, 8]], -6, 0)
    for j, (s0, s1) in enumerate(SHF):
        if j:
            io(V("W", 72 + 8 * j, 74 + 8 * j), [[s1 - s0, 2]], s0, 0)
    HR, HO, HD = V("W", 160, 296), V("W", 320, 456), V("W", 480, 616)
    io(HR, [[0, 17], [2, 8]], 0, 0)
    ts(HO, HR, c_(3), ALU.is_equal)
    ts(HD, HR, 0.0, ALU.is_gt)
    tt(HR, HO, V("W", 0, 136), mul)
    scan(V("W", 640, 776), HD, HR, 0.0)
    aff(c_(7), c_(4), scale=-63.0, bias=64.0)
    aff(V("CW", 0, 9), V("W", 647, 712, 8), scale=c_(7))
    aff(V("CT", 0, 8), V("W", 719, 776, 8), bias=c_(0))
    aff(V("CW", 6, 9, 2), V("CW", 6, 9, 2), scale=1.0 / 64)
    aff(c_(8), c_(2), bias=15.0)
    WS = V("WS", 0, 144)
    ts(WS, V("R", 0, 144), c_(8), ALU.is_equal)
    for j, m in enumerate(WN):
        aff(V(m, 0, 144), WS, scale=V("CW", j, j + 1), engs="va")
    aff(V("WM", 0, 144), V("W23", 0, 144), scale=512.0, engs="va")
    R8 = V("R", 0, 128)
    ONES, TRI, FL = m_("ONES"), m_("TRI"), V("FL", 0, 164)
    ts(m_("I32"), R8, c_(0), ALU.is_equal)
    for m, s in (("I1", 1.0), ("IA", float(A)), ("IP", float(P)), ("NI", -512.0)):
        aff(m_(m), m_("I32"), scale=s)
    aff(c_(9), c_(2), scale=-1.0, bias=-7.5)
    ab(m_("MB2"), R8, c_(9))
    ts(ONES, m_("MB2"), 8.0, ALU.is_lt)
    ts(m_("TQ"), m_("MB2"), 8.0, ALU.is_lt, -1.0, mul)
    add("tri", "g", plain(TRI, TRI), [m_("TQ")], [m_("TR0")], o=m_("TR0"), i=m_("TQ"))
    tt(TRI, m_("TR0"), m_("IP"), add_)
    io(m_("MB2"), [[0, 8], [-1, 16]], 0, 0)
    ts(m_("MB2"), m_("MB2"), e_(6), mul)
    tt(m_("TQ"), m_("MB2"), R8, add_)
    aff(c_(10), e_(6), scale=127.0, bias=1.0)
    for j, m in enumerate(MN):
        ts(m_(m), m_("TQ"), V("CT", j, j + 1), ALU.is_equal, c_(10), mul)
    aff(c_(11), e_(6), bias=-384.0)
    aff(c_(12), e_(6), bias=-256.0)
    aff(c_(13), e_(14), bias=-384.0)
    aff(c_(14), c_(5), bias=e_(8))
    ts(V("PW", 0, 256), V("PW", 0, 256), c_(2), sub)
    col, colA = V("PW", 0, 80), V("HB", 0, 80)
    io(colA, [[16, 80]], 0, 0)
    for j, b in ((0, 4096.0), (2, 1280.0)):
        aff(V("KW", 16 * j, 16 * j + 16), V("PW", 0, 16), bias=b)
    aff(V("KW", 64, 84), V("PW", 0, 20), bias=float(A - P))
    zero(FL)
    io(V("FL", 82, 83), [[0, 1]], -76, 0)
    io(V("D0", 0, 164), [[0, 164]], 1, 0)
    zero(V("D0", 82, 83))
    cp(V("THB", 0, 2), V("THI", 0, 2))
    mm([(V("P5B", 0, 2), ONES, V("THB", 0, 2))], False)
    aff(c_(16), c_(1), scale=-512.0, bias=0.5)
    aff(c_(17), c_(1), scale=-512.0, bias=-120.0)
    aff(V("TH", 0, 2), V("P5B", 0, 2), scale=-0.5, bias=c_(16), engs="a")
    aff(V("TH", 2, 4), V("P5B", 0, 2), scale=0.5, bias=-0.25, engs="a")
    aff(V("TH", 4, 6), V("P5B", 0, 2), scale=-0.5, bias=c_(17), engs="a")
    aff(V("TH", 6, 8), V("P5B", 0, 2), scale=-0.5, bias=120.25, engs="a")
    for v in (V("JA", P, QS), V("XA", A, FB), V("DA", A, KA), V("SA", 0, A), V("KT", A, KA), V("PH", P, P + 8)):
        zero(v)

    def zc(n, a, b, engs="sg"):
        while a < b:
            m = min(A, b - a)
            cp(V(n, a, a + m), V("JA", P, P + m) if SCRATCH[n][2] == BF else V("SA", 0, m), engs)
            ops[-1]["rd"].append(V("Q", 0, 8))
            a += m

    zc("TT", FB + 640, UB + 7)
    zc("TT", UB + 319, NT)
    zc("XB", A, FB)
    zc("SA", 3840, P)
    zc("SB", 0, A)
    zc("SB", 3840, P)
    zc("SF", 0, P)
    zc("SF", SS, SS + NB)

    cu = V("U", 0, 80)
    cp(V("LU", 0, 256), V("LK", 0, 256))
    ts(cu, V("LK", 0, 80), 1279, mn)
    cp(V("LW", 0, 80), V("LK", 0, 80), "vg")
    for a, b in ((0, 640), (640, A), (A, 1920), (1920, 2560), (2560, 3200), (3200, P)):
        ga(V("LX", a, b), IOT, V("LU", a // 16, b // 16))
    for a in (0, 640):
        cp(V("XA", a, a + 640), V("Q", a, a + 640), "vg")

    def primed(rnd):
        wrap(V("P3", 0, 96), V("LX", 2 * A, P), "WP")
        wrap(V("P4B", 0, 80), V("LX", A, 2 * A), "WP")
        cp(V("LW", 160, 256), V("P3", 0, 96), "av")
        cp(V("LW", 80, 160), V("P4B", 0, 80), "av")
        cp(V("F4U", 240, 256), V("LW", 240, 256))
        if rnd:
            wrap(V("P5B", 0, 80), V("LX", 0, A), "WP")
            cp(V("LU", 0, 80), V("P5B", 0, 80))
            cp(V("LU", 80, 256), V("LW", 80, 256))

    wi = [0]

    def w_():
        wi[0] += 1
        return V("W", 80 * (wi[0] - 1), 80 * wi[0])

    for rnd in range(2):
        wi[0] = 0
        X, XN = (("XA", "XB"), ("XB", "XA"))[rnd]
        RHO = "RHO"
        q, free, cand = V("LW", 0, 80), V("FL", 1, 81), V("FL", 83, 163)
        nf, ann = V("HB", 80, 160), V("HB", 160, 240)
        px = [V("PX", 80 * j, 80 * j + 80) for j in range(4)]
        xw = X0 if rnd == 0 else V("XB", 0, A)
        zc("ST", FB if rnd else 0, NT)
        zc("TT", 0, FB)
        qa, hg, qm, y1, y2, e1, z, o2 = (w_() for _ in range(8))
        for h in range(2):
            ga(V("TP", 640 * h, 640 * h + 640), V("LX", 0, A), sub_(cu, 40 * h, 40 * h + 40))
        tt(qa, q, col, sub)
        ts(free, qa, 0.0, ALU.is_equal)
        ts(nf, q, float(A), ALU.is_ge, BIG, mul)
        ts(hg, qa, 0.0, ALU.is_gt, V("TH", 6 + rnd, 7 + rnd), mul)
        aff(qm, qa, bias=-4096.0)
        w0 = wrap(V("P0", 0, 80), V("TP", 0, A), "WM", [(m_("NI"), colA), (m_("NI"), free), (m_("NI"), nf)], stop=False)
        for h in range(2):
            a, b = 640 * h, 640 * h + 640
            gat(V("DM", a, b), xw, sub_(cu, 40 * h, 40 * h + 40), V("XA", a, b), sub)
            ab(V("DA", a, b), V("DM", a, b))
        wrap(V("P0", 0, 80), V("DA", 0, A), "WS", start=False, prev=w0)
        ab(y2, V("P0", 0, 80), V("TH", 4 + rnd, 5 + rnd))
        ab(y1, V("P0", 0, 80), V("TH", rnd, rnd + 1))
        tt(cand, y2, hg, ALU.is_lt)
        ts(ann, y1, V("TH", 2 + rnd, 3 + rnd), ALU.is_lt)
        mm([(V("P2", 0, 164), ONES, FL), (V("P2", 200, 364), TRI, FL)], False)
        scan(V("SN", 0, 164), V("D0", 0, 164), V("P2", 0, 164), float(FB - 4097))
        tt(V("RK", 0, 164), V("P2", 200, 364), V("SN", 0, 164), add_)
        valF = V("RK", 1, 81)
        offu = V("U", 80, 160)
        tt(px[0], valF, col, mx)
        tt(o2, px[0], V("RK", 83, 163), mx)
        cp(offu, o2)
        primed(rnd)
        rows([(2, V("MIX", 0, A), 2, V("LX", 0, A)), (3, V("MIX", 0, A), 3, V("LX", 0, A))])
        sca(V("ST", 0, NT), offu, V("MIX", 0, A))
        if rnd == 0:
            for t, a, b, c in (("JA", 0, A, 0), ("JA", 3840, P, 3840), ("JB", 0, A, 0), ("JB", 3840, P, 3840),
                               ("RHO", 0, 2048, 0), ("RHO", 2048, P, 2048), ("RHO", P, 5632, 0)):
                dma(V(t, a, b), V("LX", P + c, P + c + b - a))
                ops[-1]["rd"].append(V("MIX", 0, 8))
        else:
            dma(V("RHO", 0, 2 * A), V("LX", P, P + 2 * A))
        su, se, so = V("ST", UB, UB + 320), V("ST", FB, FB + 640, 2), V("ST", FB + 1, FB + 640, 2)
        mm([(V("P0", 0, 320), m_("MV"), su), (V("P0", 0, 320), m_("M45"), so)], True)
        relu(V("VT", 0, 320), V("P0", 0, 320), c_(12))
        mm([(V("P1", 0, 320), m_("MU"), su), (V("P1", 0, 320), m_("M45"), se), (V("P1", 0, 320), m_("MB"), so)], True)
        relu(V("TT", UB, UB + 320), V("P1", 0, 320), c_(11))
        wrap(V("P5B", 0, 20), V("VT", 0, 320), "WV")
        vl, vu, uu = V("TW", 0, 20), V("U", 160, 180), V("U", 180, 200)
        tt(vl, V("P5B", 0, 20), V("KW", 64, 84), mn)
        ts(vu, vl, float(P), add_)
        sca(V("TT", 0, FB), vu, V("VT", 0, 320))
        mm([(V("P2", 0, 320), m_("M89"), se), (V("P2", 0, 320), m_("MC"), so), (V("P2", 0, 320), m_("ME"), su)], True)
        relu(V("TT", FB, FB + 640, 2), V("P2", 0, 320), c_(13))
        mm([(V("P6B", 0, 320), m_("M89"), so), (V("P6B", 0, 320), m_("MC"), se), (V("P6B", 0, 320), m_("MO"), su)], True)
        relu(V("TT", FB + 1, FB + 640, 2), V("P6B", 0, 320), c_(13))
        tt(e1, ann, qm, mul)
        tt(z, e1, col, add_)
        dlu = V("U", 200, 280)
        ts(dlu, z, 4096.0, add_, float(A), mn)
        if rnd == 0:
            for c in range(2):
                o = V("SA", A + 640 * c, A + 640 * c + 640)
                ga(o, V("DA", 0, KA), sub_(dlu, 40 * c, 40 * c + 40))
                cp(V("SA", 2 * A + 640 * c, 2 * A + 640 * c + 640), o, "gsa")
                cp(V("SC", 640 * c, 640 * c + 640), o, "gsa")
        else:
            slu = V("U", 280, 440)
            for h in range(2):
                ts(sub_(slu, 80 * h, 80 * h + 80), z, float(P + A + A * h), add_, float(P), mn)
                ga(V("DM", 640 * h, 640 * h + 640), V("DA", 0, KA), sub_(dlu, 40 * h, 40 * h + 40))
            for c in range(4):
                o = V("SA", A + 640 * c, A + 640 * c + 640)
                gat(o, V("PH", 0, P + 8), sub_(slu, 40 * c, 40 * c + 40), V("DM", 640 * (c % 2), 640 * (c % 2) + 640), add_)
                cp(V("SC", 640 * c, 640 * c + 640), o, "sga" if c % 2 else "gsa")
        for h in range(2):
            ga(V("TM", 640 * h, 640 * h + 640), V("TT", 0, NT), sub_(offu, 40 * h, 40 * h + 40))
        TM, ju = V("TM", 0, A), V("U", 440, 600)
        for h, bk in ((0, "P0"), (1, "P1")):
            wrap(V(bk, 0, 80), TM, "WD%d" % (h + 1), [(m_("I32"), z)])
            ts(sub_(ju, 80 * h, 80 * h + 80), V(bk, 0, 80), float(P + A + A * h), add_)
        for h in range(4):
            ga(V("JA", A + 640 * h, A + 640 * h + 640), V("LX", 0, 2 * P), sub_(ju, 40 * h, 40 * h + 40))
        l4u = V("U", 600, 680)
        wrap(V("P2", 0, 80), TM, "WD3", [(m_("I1"), colA), (m_("IP"), ann)])
        ts(l4u, V("P2", 0, 80), c_(1), add_)
        if rnd:
            aff(V("PL", 0, 80), V("P2", 0, 80), bias=c_(1))
        ga(V("TP", 0, A), V("LX", 0, 2 * P), l4u)
        wrap(V("P2", 0, 80), V("TP", 0, A), "WP")
        cp(V("F4U", 0, 80), V("P2", 0, 80))
        if rnd == 0:
            cp(V("PL", 0, 80), V("P2", 0, 80), "av")
        spec = V("P6B", 0, 80)
        wrap(spec, TM, "WN", [(m_("I1"), ann)])
        xm, xlu = w_(), V("U", 680, 760)
        for h in range(2):
            tt(V("CL", 80 * h, 80 * h + 80), col, V("LW", 80 + 80 * h, 160 + 80 * h), sub)
            tt(V("TW", 80 * h, 80 * h + 80), spec, V("CL", 80 * h, 80 * h + 80), mul)
        tt(px[1], spec, valF, mul)
        if rnd:
            aff(V("HB", 240, 320), spec, scale=float(PO), bias=float(A), engs="a")
            aff(V("HB", 320, 400), spec, scale=float(P - 2 * A), bias=float(2 * A), engs="a")
            mm([(V("P5B", 0, 80), m_("I1"), colA), (V("P5B", 0, 80), m_("I1"), V("HB", 240, 320))], True)
            mm([(V("P5B", 80, 160), m_("I1"), colA), (V("P5B", 80, 160), m_("I1"), V("HB", 320, 400))], True)
            aff(V("PL", 80, 160), V("P5B", 0, 80), bias=c_(1))
            ts(V("P5U", 160, 240), V("P5B", 80, 160), c_(1), add_, float(2 * A), sub)
        tt(xm, px[1], col, mx)
        cp(xlu, xm)
        wrap(V("P3", 0, 80), TM, "WD3", [(m_("IA"), ann), (m_("I32"), V("LW", 80, 160)), (m_("I32"), V("TW", 0, 80))])
        wrap(V("P3", 80, 160), TM, "WD4", [(m_("IA"), ann), (m_("IA"), ann), (m_("I32"), V("LW", 160, 240)), (m_("I32"), V("TW", 80, 160))])
        cp(V("F4U", 80, 240), V("P3", 0, 160))
        if rnd == 0:
            cp(V("PL", 80, 160), V("P3", 0, 80), "av")
        pb = V("LW", 240, 256) if rnd == 0 else V("PW", 240, 256)
        wrap(V("P4B", 0, 20), V("VT", 0, 320), "W23")
        cp(uu, V("P4B", 0, 20))
        ga(V("X1", 0, 320), V(X, 0, A), uu)
        ga(V(X, FB + 1, FB + 640, 2), V("DA", 0, A), uu)
        gat(V("S1", 0, 320), V(X, 0, FB), vu, V("X1", 0, 320), add_)
        ts(V("PX", 160, 480), V("S1", 0, 320), 16.0, ALU.is_ge, -16.0, mul)
        tt(V(X, FB, FB + 640, 2), V("PX", 160, 480), V("S1", 0, 320), add_)
        ga(V(XN, 0, A), V(X, 0, FB + 640), xlu)
        banks = ("P0", "P1", "P4B", "P5B")
        for s in range(5):
            jx, jy, jo = (("JA", "JB", A), ("JB", "JA", A), ("JA", "JB", A), ("JB", "JA", A), ("JA", "LX", 2 * P))[s]
            sx, sy, so_ = (("SA", "SB", A), ("SB", "SA", A), ("SA", "SB", A), ("SB", "SA", A), ("SA", "SF", P))[s]
            for h in range(2):
                bk = banks[(2 * s + h) % 4]
                wrap(V(bk, 0, 80), V(jx, A + A * h, 2 * A + A * h), "W23")
                cp(V("JU", 160 * s + 80 * h, 160 * s + 80 * h + 80), V(bk, 0, 80))
            for h in range(2):
                ga(V(jy, jo + A * h, jo + A + A * h), V(jx, 0, P), V("JU", 160 * s + 80 * h, 160 * s + 80 * h + 80), "a")
            for a in range(0, 2 * A, SP):
                b = a % A if rnd == 0 and s == 0 else a
                gat(V(sy, so_ + a, so_ + a + SP), V(sx, 0, P), V("JU", 160 * s + a // 16, 160 * s + (a + SP) // 16), V("SC", b, b + SP), add_)
            for c in range(4 if s < 4 else 0):
                cp(V("SC", 640 * c, 640 * c + 640), V(sy, A + 640 * c, A + 640 * c + 640), "sga" if c % 2 else "gsa")
        JW, SW = V("LX", P, 2 * P + 2 * A), V("SF", 0, SS)
        ga(V("KT", KB, KB + NB), JW, V("F4U", 240, 256), "a")
        for h in range(2):
            ga(V("KT", 640 * h, 640 * h + 640), JW, V("F4U", 40 * h, 40 * h + 40))
        wrap(V("P0", 0, 16), V("KT", KB, KB + NB), "W23")
        atu = V("U", 760, 776)
        ts(atu, V("P0", 0, 16), float(A), mn)
        cp(V("L5U", 240, 256), V("P0", 0, 16))
        cp(V("AW", 0, 16), V("P0", 0, 16), "av")
        aff(V("AW", 16, 32), V("PW", 0, 16), bias=float((SS, QS)[rnd]))
        gat(V("EQ", 0, NB), V("KT", 0, KA), atu, V("LX", P + 3840, 2 * P), ALU.is_equal)
        wrap(V("P1", 0, 16), V("EQ", 0, NB), "W23")
        SF, RF, SX, RX, RP = ("%s%d" % (s, rnd) for s in ("SF", "RF", "SX", "RX", "RP"))
        for j in range(2):
            ts(V(SF, 16 * j, 16 * j + 16), V("P1", 0, 16), 65.0, ALU.not_equal, (BIG, -BIG)[j], mul)
        send(V(RF, 0, 32), V(SF, 0, 32), rnd)
        tt(V("AW", 48, 80), V("AW", 0, 32), V(SF, 0, 32), add_)
        ga(V(SX, 0, NB), V(XN, 0, KA), atu)
        send(V(RX, 0, NB), V(SX, 0, NB), rnd)
        if rnd == 0:
            own = V("SP0", 0, NB)
            ga(own, SW, V("F4U", 240, 256))
        else:
            own = V("Q", 3840, P)
            gat(own, SW, V("LU", 240, 256), V("PH", 3840, P), add_)
            ts(own, own, 15, band)
        send(V(RP, 0, NB), own, rnd)
        for h in range(2):
            ga(V("KT", KA + A * h, KA + A * h + A), JW, V("F4U", 80 + 80 * h, 160 + 80 * h))
        wrap(V("P2", 0, 80), V("KT", 0, A), "W23")
        wrap(V("P3", 0, 80), V("KT", KA, KA + A), "W23")
        wrap(V("P4B", 0, 80), V("KT", KA + A, KB), "W23")
        cp(V("K4", 0, 80), V("P2", 0, 80), "av")
        cp(V("K4", 80, 160), V("P3", 0, 80), "av")
        cp(V("L5U", 160, 240), V("P4B", 0, 80))
        aff(V("VR", 0, NB), V("KT", KB, KB + NB), bias=c_(14))
        dlt, d1, d2, k2 = w_(), w_(), w_(), w_()
        tt(dlt, V("P3", 0, 80), V("K4", 0, 80), sub)
        tt(d1, V("PL", 80, 160), V("PL", 0, 80), sub)
        aff(k2, V("PL", 80, 160), scale=-1.0, bias=float((SS, QS)[rnd] - 3840))
        tt(d2, V("P2", 0, 80), k2, add_)
        if rnd == 0:
            ga(V("PH", 2 * A, 3 * A), SW, V("F4U", 160, 240))
        else:
            for c in range(6):
                o = V("Q", 640 * c, 640 * c + 640)
                gat(o, SW, V("LU", 40 * c, 40 * c + 40), V("PH", 640 * c, 640 * c + 640), add_)
                ts(o, o, 15, band)
                cp(V("JA", 640 * c, 640 * c + 640), o, "gv")
            cp(V("JA", 3840, P), own, "gv")
            for a in (2560, 3200):
                ga(V("JB", a, a + 640), V("JA", 2 * A, QS), V("P5U", a // 16, a // 16 + 40))
                dma(("yp", a, a + 640, 1), V("JB", a, a + 640))
        tt(V("PX", 480, 512), V("AW", 48, 80), V(RF, 0, 32), add_)
        tt(V("BW", 64, 80), V("PX", 480, 496), V("KW", 0, 16), mn)
        cp(V("OU", 0, 16), V("BW", 64, 80))
        sca(V(RHO, 0, P + NB), V("OU", 0, 16), V("VR", 0, NB))
        sca(V(RHO, A, 5632), V("OU", 0, 16), V("KT", KB, KB + NB))
        wrap(V("P0", 0, 80), V(RHO, 0, A), "WF")
        tt(V("BW", 96, 112), V("PX", 480, 496), V("KW", 32, 48), mn)
        tt(V("BW", 112, 128), V("PX", 496, 512), pb, mx)
        cp(V("OU", 32, 64), V("BW", 96, 128))
        sca(V(XN, 0, 1536), V("OU", 32, 48), V(RX, 0, NB))
        sw = V("P0", 0, 80)
        t0, t1, t2 = w_(), V("CL", 0, 80), V("CL", 80, 160)
        tt(t0, sw, dlt, mul)
        tt(px[0], t0, V("K4", 0, 80), add_)
        cp(V("L5U", 0, 80), px[0])
        tt(px[1], V("K4", 80, 160), t0, sub)
        cp(V("L5U", 80, 160), px[1])
        tt(t1, sw, d1, mul)
        tt(t2, sw, d2, mul)
        tt(V("PX", 160, 320), V("CL", 0, 160), V("PL", 0, 160), add_)
        cp(V("P5U", 0, 160), V("PX", 160, 320))
        RW = V(RHO, 0, P)
        if rnd == 0:
            for a in (0, 640):
                cp(V("XA", a, a + 640), V("XB", a, a + 640), "gsva")
            tt(V("SF", SS, SS + NB), own, V(RP, 0, NB), add_)
            for h in range(2):
                ga(V("LX", 640 * h, 640 * h + 640), RW, V("L5U", 40 * h, 40 * h + 40))
            wrap(V("P1", 0, 80), V("LX", 0, A), "W23")
            ts(cu, V("P1", 0, 80), 1279.0, mn)
            cp(V("LW", 0, 80), V("P1", 0, 80), "va")
            for a, b in ((2560, 3328), (3328, P), (A, 1920), (1920, 2560)):
                ga(V("LX", a, b), RW, V("L5U", a // 16, b // 16))
            SW = V("SF", 0, SS + NB)
            for a in (A, 1920, 0, 640):
                ga(V("PH", a, a + 640), SW, V("P5U", a // 16, a // 16 + 40))
            ga(V("PH", 3840, P), SW, V("OU", 48, 64))
        else:
            dma(("yx", 0, A, 1), V(XN, 0, A))
            qs = V("Q", P, P + NB)
            tt(qs, own, V(RP, 0, NB), add_)
            ts(qs, qs, 15, band)
            cp(V("JA", QS, QS + NB), qs, "vg")
            for a, b in ((3840, P), (0, 640), (640, A), (A, 1920), (1920, 2560)):
                ga(V("JB", a, b), V("JA", 0, QS + NB), V("P5U", a // 16, b // 16) if a < 3840 else V("OU", 48, 64))
                dma(("yp", a, b, 1), V("JB", a, b))
            for a, b in ((2560, 3328), (3328, P), (0, 768), (768, A), (A, 2048), (2048, 2560)):
                ga(V("LX", a, b), RW, V("L5U", a // 16, b // 16))
            for n, i in enumerate(list(range(10, 16)) + list(range(10))):
                add("blk", "p", {"p": 0.02 + 256 * PCY}, [V("LX", 256 * i, 256 * i + 256), V("W23", 0, 144)], [V("P1", 0, 256)],
                    i=i, start=n == 0, stop=n == 15)
            cp(V("RP0", 0, 256), V("P1", 0, 256), "a")
            dma(("yl", 0, P, 1), V("RP0", 0, 256))
    return ops


def graph(ops):
    seen = {}
    for n, o in enumerate(ops):
        dep = set()
        acc = [(r, False) for r in o["rd"]] + [(w, True) for w in o["wr"]]
        for v, w in acc:
            for m, a, b, pw in seen.get(v[0], []):
                if ((w or pw) and a < v[2] and v[1] < b) or (v[0] in PSUM and (ops[m]["engs"] != o["engs"] or len(o["engs"]) > 1)):
                    dep.add(m)
        for v, w in acc:
            lst = seen.setdefault(v[0], [])
            if w and v[3] == 1 and (v[0] not in PSUM or v[0] == "PX"):
                lst[:] = [x for x in lst if not (v[1] <= x[1] and x[2] <= v[2])]
            lst.append((n, v[1], v[2], w))
        dep.discard(n)
        o["dep"] = sorted(dep)


def replay(seq, pred, c, la, eng):
    n = len(seq)
    fin = [0.0] * n
    bind = [-1] * n
    free = [0.0] * 5
    prev = [-1] * 5
    end, last, tot = 0.0, -1, 0.0
    for i in seq:
        e = eng[i]
        st = free[e]
        b = prev[e]
        for d in pred[i]:
            if fin[d] > st:
                st = fin[d]
                b = d
        bind[i] = b
        st += c[i]
        free[e] = st
        prev[e] = i
        st += la[i]
        fin[i] = st
        tot += st
        if st > end:
            end, last = st, i
    return end, tot, fin, bind, last


def greedy(c, la, pred, succ, pr, eng, back):
    n = len(c)
    left = [len(x) for x in pred]
    rdy = list(la) if back else [0.0] * n
    ready = [[i for i in range(n) if left[i] == 0 and eng[i] == e] for e in range(5)]
    free = [0.0] * 5
    nxt = {e: min([rdy[i] for i in ready[e]]) for e in range(5) if ready[e]}
    seq, fin = [], [0.0] * n
    for _ in range(n):
        e = min(nxt, key=nxt.get)
        t0 = nxt[e]
        i = max([(pr[j], j) for j in ready[e] if rdy[j] <= t0 + SLACK])[1]
        ready[e].remove(i)
        free[e] = max(t0, rdy[i]) + c[i]
        if ready[e]:
            nxt[e] = max(free[e], min([rdy[j] for j in ready[e]]))
        else:
            del nxt[e]
        fin[i] = free[e] if back else free[e] + la[i]
        seq.append(i)
        for s in succ[i]:
            rdy[s] = max(rdy[s], fin[i] + la[s] if back else fin[i])
            left[s] -= 1
            if left[s] == 0:
                x = eng[s]
                ready[x].append(s)
                nxt[x] = min(nxt.get(x, 1e9), max(rdy[s], free[x]))
    return seq, fin


PLAN = {}
ENG = "vapgs"


def plan():
    if not PLAN:
        ops = build()
        graph(ops)
        n = len(ops)
        anc, pred, succ = [0] * n, [], [[] for _ in range(n)]
        for i, o in enumerate(ops):
            cover = 0
            for d in o["dep"]:
                cover |= anc[d]
            pred.append([d for d in o["dep"] if not cover >> d & 1])
            for d in pred[i]:
                succ[d].append(i)
                cover |= 1 << d
            anc[i] = cover
        alt = [[ENG.index(x) for x in o["engs"]] for o in ops]
        eng = [x[0] for x in alt]
        c = [ops[i]["cost"][ENG[eng[i]]] for i in range(n)]
        la = [ops[i]["lat"].get(ENG[eng[i]], 0.0) + LAT for i in range(n)]
        pr = [0.0] * n
        for i in range(n - 1, -1, -1):
            pr[i] = c[i] + la[i] + max([pr[s] for s in succ[i]] + [0.0])
        rs = np.random.RandomState(SEED)
        seq, fin = greedy(c, la, pred, succ, pr, eng, False)
        flex = [i for i in range(n) if len(alt[i]) > 1]
        for t in range(TRIES):
            i = flex[int(rs.randint(len(flex)))]
            oe, oc, ol = eng[i], c[i], la[i]
            ne = alt[i][int(rs.randint(len(alt[i])))]
            eng[i], c[i], la[i] = ne, ops[i]["cost"][ENG[ne]], ops[i]["lat"].get(ENG[ne], 0.0) + LAT
            s2, f2 = greedy(c, la, pred, succ, greedy(c, la, succ, pred, fin, eng, True)[1], eng, False)
            if max(f2) <= max(fin) + 0.5 * (1.0 - t / TRIES) * rs.uniform():
                seq, fin = s2, f2
            else:
                eng[i], c[i], la[i] = oe, oc, ol
        end, tot, fin, bind, last = replay(seq, pred, c, la, eng)
        cur = end + 0.05 * tot / n
        best = (end, list(seq), list(eng))
        pos = [0] * n
        chain = None
        rnd = rs.uniform(size=(STEPS, 7)).tolist()
        for t in range(STEPS):
            if chain is None:
                chain = []
                x = last
                while x >= 0:
                    chain.append(x)
                    x = bind[x]
                for p, i in enumerate(seq):
                    pos[i] = p
            u0, u1, u2, u3, u4, u5, u6 = rnd[t]
            i = chain[int(u1 * len(chain))] if u0 < 0.6 else int(u1 * n)
            p, oe = pos[i], eng[i]
            ne = alt[i][int(u3 * len(alt[i]))] if u2 < 0.35 else oe
            w = 1 + int(40 * u4 * u4 * u4) if u2 > 0.1 else 0
            q = max(p - w, max([pos[d] for d in pred[i]] + [-1]) + 1) if u5 < 0.5 else min(p + w, min([pos[s] for s in succ[i]] + [n]) - 1)
            if q == p and ne == oe:
                continue
            s2 = seq[:p] + seq[p + 1:]
            s2.insert(q, i)
            oc, ol = c[i], la[i]
            eng[i], c[i], la[i] = ne, ops[i]["cost"][ENG[ne]], ops[i]["lat"].get(ENG[ne], 0.0) + LAT
            e2, t2, f2, b2, l2 = replay(s2, pred, c, la, eng)
            v = e2 + 0.05 * t2 / n
            if v <= cur or u6 < math.exp((cur - v) / (HEAT * (1.0 - t / STEPS) ** 2 + 1e-4)):
                seq, cur, bind, last, chain = s2, v, b2, l2, None
                if e2 < best[0]:
                    best = (e2, list(seq), list(eng))
            else:
                eng[i], c[i], la[i] = oe, oc, ol
        PLAN["ops"], PLAN["end"], PLAN["seq"], PLAN["eng"], PLAN["pred"] = ops, best[0], best[1], best[2], pred
    return PLAN["ops"], [(i, ENG[PLAN["eng"][i]]) for i in PLAN["seq"]]


def rank_program(g, core, T, topo):
    rank = T.rank_of(core)
    if rank is None:
        return
    ops, order = plan()
    Q = {"v": g.vector, "a": g.scalar, "p": g.tensor, "g": g, "s": g.sync}
    CS = {"v": "cv", "a": "ca", "p": "cp", "g": "cg"}

    def ap(v):
        if not isinstance(v, tuple):
            return v
        if v[0] == "yl":
            return T.yl[:]
        return T[v[0]][:, v[1]:v[2]:v[3]] if v[3] != 1 else T[v[0]][:, v[1]:v[2]]

    count = {"cv": 0, "ca": 0, "cp": 0, "cg": 0}
    total = {}
    known = {e: {} for e in Q}
    done = {}
    nd = 0
    for i, e in order:
        o = ops[i]
        kind = o["kind"]
        k = {n: ap(v) for n, v in o["k"].items()}
        q = Q[e]
        kn = known[e]
        need = {}
        for d in o["dep"]:
            if (kind == "blk" and ops[d]["kind"] == "blk") or d == k.get("prev"):
                continue
            sem, val, snap = done[d]
            if need.get(sem, (0, None))[0] < val:
                need[sem] = (val, snap)
        for sem in sorted(need, key=lambda s: -len(need[s][1])):
            val, snap = need[sem]
            if kn.get(sem, 0) < val:
                q.wait_ge(T.sem[sem], val)
                kn[sem] = val
                for s2, v2 in snap.items():
                    if kn.get(s2, 0) < v2:
                        kn[s2] = v2
        if e == "s" or "dma" in k:
            sem = "d%d" % nd
            nd += 1
            if "rows" in k:
                for ro, vo, ri, vi in k["rows"]:
                    q.dma_start(T[vo[0]][ro:128:16, vo[1]:vo[2]], T[vi[0]][ri:128:16, vi[1]:vi[2]]).then_inc(T.sem[sem], 16)
            else:
                q.dma_start(k["o"], k["i"]).then_inc(T.sem[sem], 16)
            total[sem] = 16 * len(k["rows"]) if "rows" in k else 16
            done[i] = (sem, total[sem], dict(kn))
            continue
        if kind == "send":
            peer = T.cores[rank ^ XM[k["rnd"]]]
            rid, pid, _se = topo.addr(peer)
            g.remote_dma(k["o"], k["i"], T.sem[k["sem"]], T.sem.sent, pid, rid, topo.mask(core, peer))
            total["sent"] = total.get("sent", 0) + len(topo.engines(core, peer))
            total[k["sem"]] = len(topo.engines(peer, core))
            done[i] = (k["sem"], total[k["sem"]], {})
            continue
        if kind in ("ga", "gat", "sca"):
            ind = k["w"].indirect(k["l"])
        if kind == "ts":
            if k["op1"] is None:
                r = q.tensor_scalar(k["o"], k["i"], k["s1"], None, k["op0"])
            else:
                r = q.tensor_scalar(k["o"], k["i"], k["s1"], k["s2"], k["op0"], k["op1"])
        elif kind == "tt":
            r = q.tensor_tensor(k["o"], k["a"], k["b"], k["op"])
        elif kind == "cp":
            if e == "g":
                r = q.affine_select(k["o"], k["i"], [[0, width(o["k"]["o"])]], ALU.is_ge, 0.0, 0, 0)
            else:
                r = q.tensor_copy(k["o"], k["i"]) if e == "v" else q.activation(k["o"], k["i"], ACT.Copy)
        elif kind == "aff":
            if e == "a":
                r = q.activation(k["o"], k["i"], ACT.Identity, bias=k["bias"], scale=k["scale"])
            elif o["k"]["scale"] == 1.0:
                r = q.tensor_scalar(k["o"], k["i"], k["bias"], None, ALU.add)
            else:
                r = q.tensor_scalar(k["o"], k["i"], k["scale"], k["bias"], ALU.mult, ALU.add)
        elif kind == "abs":
            r = q.activation(k["o"], k["i"], ACT.Abs, bias=k["bias"])
        elif kind == "relu":
            if e == "a":
                r = q.activation(k["o"], k["i"], ACT.Relu, bias=k["bias"])
            else:
                r = q.tensor_scalar(k["o"], k["i"], k["bias"], 0.0, ALU.add, ALU.max)
        elif kind == "tri":
            r = q.affine_select(k["o"], k["i"], [[-1, 128]], ALU.is_gt, 0.0, 0, 1)
        elif kind == "ga":
            r = q.activation(k["o"], ind, ACT.Copy) if e == "a" else q.tensor_copy(k["o"], ind)
        elif kind == "gat":
            r = q.tensor_tensor(k["o"], ind, k["b"], k["op"])
        elif kind == "sca":
            r = q.tensor_copy(ind, k["i"])
        elif kind == "wrap":
            t = o["k"]["t"]
            ms = [(ap(l), ap(rr)) for l, rr in k["extra"]] + [(T[k["m"]][:, 15 - j:143 - j], T[t[0]][:, t[1] + j:t[2]:16]) for j in range(16)]
            for j, (l, rr) in enumerate(ms):
                r = q.matmul(k["o"], l, rr, k["start"] and j == 0, k["stop"] and j == len(ms) - 1)
        elif kind == "blk":
            j = k["i"]
            r = q.matmul(T.P1[:, 0:256], T.W23[:, 15 - j:143 - j], T.LX[:, 256 * j:256 * j + 256], k["start"], k["stop"])
        elif kind == "mm":
            for j, (oo, l, rr) in enumerate(k["items"]):
                r = q.matmul(ap(oo), ap(l), ap(rr), j == 0 or not k["acc"], j == len(k["items"]) - 1 or not k["acc"])
        elif kind == "scan":
            r = q.tensor_tensor_scan(k["o"], k["a"], k["b"], k["init"], ALU.mult, ALU.add)
        elif kind == "ms" and e == "v":
            r = q.memset(k["o"], 0.0)
        elif kind == "ms":
            r = q.iota(k["o"], [[0, width(o["k"]["o"])]], 0, 0, allow_small_or_imprecise_dtypes=True)
        elif SCRATCH[o["k"]["o"][0]][2] == I32:
            r = q.iota(k["o"], k["pat"], k["base"], k["cm"])
        else:
            r = q.iota(k["o"], k["pat"], k["base"], k["cm"], allow_small_or_imprecise_dtypes=True)
        sem = CS[e]
        r.then_inc(T.sem[sem], 1)
        count[sem] += 1
        done[i] = (sem, count[sem], dict(kn))
    total.update(count)
    for sem in sorted(total):
        if total[sem] and known["g"].get(sem, 0) < total[sem]:
            g.wait_ge(T.sem[sem], total[sem])
